import numpy as np
import ml_dtypes


def mxq(x, axis, fmt="e4m3"):
    dtype, down = {"e4m3": (ml_dtypes.float8_e4m3fn, 7), "e5m2": (ml_dtypes.float8_e5m2, 14)}[fmt]
    v = np.moveaxis(np.asarray(x, np.float32).astype(ml_dtypes.bfloat16).astype(np.float64), axis, -1)
    blocks = v.reshape(v.shape[:-1] + (-1, 32))
    amax = np.abs(blocks).max(-1, keepdims=True)
    byte = np.maximum(np.where(amax > 0, np.frexp(amax)[1] - 1 + 127, 0) - down, 1)
    scale = np.exp2(byte - 127.0)
    codes = (blocks / scale).astype(np.float32).astype(dtype).astype(np.float64)
    return np.moveaxis((codes * scale).reshape(v.shape), -1, axis)


WIDE = False


def mx_kscale(k):
    if not WIDE:
        return np.ones(k)
    levels = np.array([10, -10, 5, -5, 0])
    if k % 512:
        return np.exp2(np.random.permutation(np.resize(levels, k // 32))).repeat(32)
    a = np.empty((k // 512, 16))
    for p in range(k // 512):
        a[p, :8] = np.random.permutation(np.resize(levels, 8))
        for g in range(8):
            far = levels[np.abs(levels - a[p, g]) >= 10]
            a[p, g + 8] = far[np.random.randint(len(far))]
    return np.exp2(a.ravel()).repeat(32)


def f64(x):
    return np.asarray(x).astype(np.float64)


def striped(idx):
    return np.tile(np.asarray(idx).reshape(-1, 16).T, (8, 1)).astype(np.uint16)


def unstriped(offs):
    return offs[:16].T.reshape(-1).astype(np.int64)


def striped8(idx):
    return np.asarray(idx).reshape(8, -1, 16).transpose(0, 2, 1).reshape(128, -1).astype(np.uint16)


def unstriped8(offs):
    return offs.reshape(8, 16, -1).transpose(0, 2, 1).reshape(8, -1).astype(np.int64)


def pick8(x, idx, run):
    r = np.arange(len(x))
    return x[r[:, None], idx[r % (8 * run) // run]]


E2M1 = np.array([0.0, 0.5, 1.0, 1.5, 2.0, 3.0, 4.0, 6.0, -0.0, -0.5, -1.0, -1.5, -2.0, -3.0, -4.0, -6.0])


def pack_weight(w, fmt):
    k, n = w.shape
    w = f64(np.asarray(w, np.float32).astype(ml_dtypes.bfloat16)).reshape(k // 32, 32, n)
    amax = np.abs(w).max(1)
    if fmt == "e4m3":
        byte = np.frexp(amax)[1] - 1 + 127 - 7
    else:
        mant, ex = np.frexp(amax / 6.0)
        byte = np.where(mant > 0.5, ex, ex - 1) + 127
    byte = np.clip(np.where(amax > 0, byte, 1), 1, 254)
    scaled = (w * np.exp2(127.0 - byte)[:, None, :]).reshape(k, n).astype(np.float32)
    by_word = np.ascontiguousarray(scaled.reshape(k // 512, 128, 4, n).transpose(0, 1, 3, 2))
    if fmt == "e4m3":
        words = by_word.astype(ml_dtypes.float8_e4m3fn).view(np.uint8)
    else:
        c = by_word.astype(ml_dtypes.float4_e2m1fn).view(np.uint8) & 0xF
        words = (c[..., 0::2] | (c[..., 1::2] << 4)).reshape(k // 512, 128, 2 * n)
    return np.ascontiguousarray(words), np.ascontiguousarray(byte.astype(np.uint8).reshape(k // 512, 16, n))


def unpack_weight(words, scales, fmt):
    g, _, n = scales.shape
    words = np.ascontiguousarray(words).reshape(g, 128, n, -1)
    if fmt == "e4m3":
        vals = words.view(ml_dtypes.float8_e4m3fn).astype(np.float64)
    else:
        nib = np.empty((g, 128, n, 4), np.uint8)
        nib[..., 0::2] = words & 0xF
        nib[..., 1::2] = words >> 4
        vals = E2M1[nib]
    vals = vals * np.repeat(np.exp2(scales.astype(np.float64) - 127.0), 8, axis=1)[..., None]
    return vals.transpose(0, 1, 3, 2).reshape(g * 512, n)


D, C, T, I, Q, E = 512, 1024, 2048, 512, 128, 512


def setup_inputs():
    n = np.random.standard_normal
    idx = np.stack([np.random.randint(0, C, I) for _ in range(8)])
    idx2 = np.random.permutation(T)[:I]
    fd = mx_kscale(D)
    fi = mx_kscale(I)
    bookp = pack_weight(n((D, C)) / fd[:, None], "e4m3")
    finep = pack_weight(n((D, T)) * 0.5 / fd[:, None], "e4m3")
    return {
        "query": (n((D, Q)) * 0.25 / np.sqrt(D) * fd[:, None]).astype(np.float32),
        "book_words": bookp[0],
        "book_scales": bookp[1],
        "fine_words": finep[0],
        "fine_scales": finep[1],
        "size": (np.random.uniform(0.5, 2.0, (1, I)) * fi).astype(np.float32),
        "vals": (n((I, E)) / fi[:, None]).astype(np.float32),
        "offs": striped8(idx),
        "offs2": striped(idx2),
    }


def reference(query, book_words, book_scales, fine_words, fine_scales, size, vals, offs, offs2):
    idx = unstriped8(offs)
    idx2 = unstriped(offs2)
    booku = unpack_weight(book_words, book_scales, "e4m3")
    fineu = unpack_weight(fine_words, fine_scales, "e4m3")
    queryq = mxq(f64(query), 0, "e4m3")
    bookidxg = pick8(booku, idx, 64)
    fineidx2g = fineu[:, idx2]
    a = queryq.T @ bookidxg + queryq.T @ fineidx2g
    p = np.exp(a - np.max(a, axis=1, keepdims=True))
    w = p * f64(size) / np.sum(p, axis=1, keepdims=True)
    wt = w.T
    wtq = mxq(wt, 0, "e4m3")
    valsq = mxq(f64(vals), 0, "e4m3")
    o = wtq.T @ valsq
    return o

@@ -1,0 +1,140 @@
+from contextlib import ExitStack
+
+import concourse.mybir as mybir
+from concourse.masks import make_identity
+
+D, C, T, I, Q, E = 512, 1024, 2048, 512, 128, 512
+FLOPS = 2 * Q * I * (2 * D + E)
+
+F32 = mybir.dt.float32
+BF16 = mybir.dt.bfloat16
+I32 = mybir.dt.int32
+U32 = mybir.dt.uint32
+U16 = mybir.dt.uint16
+U8 = mybir.dt.uint8
+FP8X4 = mybir.dt.float8_e4m3fn_x4
+ALU = mybir.AluOpType
+ACT = mybir.ActivationFunctionType
+P = 128
+HALF = E // 2
+QUART = E // 4
+
+
+def tile_attend_pqresid_kernel(tc, query, book_words, book_scales, fine_words, fine_scales, size, vals, offs, offs2, out):
+    nc = tc.nc
+    with ExitStack() as ctx:
+        sb = ctx.enter_context(tc.tile_pool(name="sb", bufs=1))
+        ps = ctx.enter_context(tc.psum_pool(name="ps", bufs=1))
+
+        book_list = sb.tile([P, I // 16], U16, name="book_list")
+        fine_list = sb.tile([P, I // 16], U16, name="fine_list")
+        bs_win = sb.tile([P, C], U8, name="bs_win", align_bytes=64)
+        fs_win = sb.tile([P, T], U8, name="fs_win", tag="first", align_bytes=64)
+        bw_win = sb.tile([P, C], I32, name="bw_win", tag="second", align_bytes=64)
+        fw_win = sb.tile([P, T], I32, name="fw_win", align_bytes=64)
+        q_raw = sb.tile([P, 4, Q], F32, name="q_raw", align_bytes=64)
+        size_col = sb.tile([P, 4], F32, name="size_col")
+
+        nc.vector.memset(bs_win[:].bitcast(I32), 0)
+        nc.vector.memset(fs_win[:].bitcast(I32), 0)
+        nc.sync.dma_start(book_list[:], offs)
+        nc.sync.dma_start(fine_list[:], offs2)
+        for w in range(2):
+            nc.scalar.dma_start(bs_win[w:P:16, :].bitcast(I32), book_scales[0, w:16:2, :].bitcast(I32))
+        nc.sync.dma_start(bw_win[:], book_words[0].rearrange("p c t -> p (c t)").bitcast(I32))
+        nc.sync.dma_start(q_raw[:], query.rearrange("(p j) q -> p j q", j=4))
+        nc.sync.dma_start(fw_win[:], fine_words[0].rearrange("p c t -> p (c t)").bitcast(I32))
+        for x, queue in enumerate((nc.scalar, nc.scalar, nc.gpsimd, nc.gpsimd)):
+            queue.dma_start(fs_win[32 * x:32 * x + 4, :].bitcast(I32), fine_scales[0, 4 * x:4 * x + 4, :].bitcast(I32))
+        nc.sync.dma_start(size_col[:], size.rearrange("o (s t) -> (o s) t", t=4))
+
+        ident = sb.tile([P, P], F32, name="ident")
+        make_identity(nc, ident[:])
+        bs_pl = sb.tile([P, I], U8, name="bs_pl", align_bytes=64)
+        warm = sb.tile([P, 1], F32, name="warm")
+        nc.vector.memset(warm[:], 0.0)
+        warm_out = sb.tile([P, 1], F32, name="warm_out")
+        nc.scalar.activation(warm_out[:], warm[:], ACT.Exp)
+
+        bs_g = sb.tile([P, I], U8, name="bs_g", align_bytes=64)
+        fs_g = sb.tile([P, I], U8, name="fs_g", align_bytes=64)
+        bw_g = sb.tile([P, I], I32, name="bw_g", align_bytes=64)
+        fw_g = sb.tile([P, I], I32, name="fw_g", align_bytes=64)
+        nc.vector.tensor_copy(bs_g[:], bs_win[:].indirect(book_list[:]))
+        nc.vector.tensor_copy(bs_pl[:].bitcast(I32), bs_g[:].bitcast(I32))
+        for w in range(2):
+            nc.scalar.dma_start(bs_pl[2 + w:P:32, :].bitcast(I32), bs_g[16 + w:P:32, :].bitcast(I32))
+        nc.vector.tensor_copy(bw_g[:].bitcast(U32), bw_win[:].bitcast(U32).indirect(book_list[:]))
+        nc.vector.tensor_copy(fs_g[:], fs_win[:].indirect(fine_list[:]))
+        vals_rows = vals.rearrange("(p j) e -> p j e", j=4)
+        v_raw = []
+        for h, tag in enumerate(("second", "first")):
+            v_raw.append(sb.tile([P, 4, HALF], F32, name="v_raw%d" % h, tag=tag, align_bytes=64))
+            nc.sync.dma_start(v_raw[h][:], vals_rows[:, :, h * HALF:(h + 1) * HALF])
+
+        size_ps = ps.tile([P, 2, 2, P], F32, name="size_ps")
+        for u in range(2):
+            for e in range(2):
+                t = 2 * u + e
+                nc.tensor.transpose(size_ps[:, e, u, :], size_col[:, t:t + 1].to_broadcast([P, P]), ident[:])
+
+        q_bf = sb.tile([P, Q, 4], BF16, name="q_bf", align_bytes=64)
+        nc.scalar.copy(q_bf[:], q_raw[:].rearrange("p j q -> p q j"))
+        q_codes = sb.tile([P, Q], U32, name="q_codes", align_bytes=64)
+        q_scales = sb.tile([P, Q], U8, name="q_scales", align_bytes=64)
+        nc.vector.quantize_mx(out=q_codes[:].bitcast(FP8X4), scales=q_scales[:], in_=q_bf[:].rearrange("p q j -> p (q j)"))
+
+        nc.vector.tensor_copy(fw_g[:].bitcast(U32), fw_win[:].bitcast(U32).indirect(fine_list[:]))
+
+        scores = ps.tile([P, I], F32, name="scores")
+        nc.tensor.matmul_mx(out=scores[:], lhsT=q_codes[:].bitcast(FP8X4), lhsT_scale=q_scales[:],
+                            rhs=bw_g[:].bitcast(FP8X4), rhs_scale=bs_pl[:], start=True, stop=False)
+        nc.tensor.matmul_mx(out=scores[:], lhsT=q_codes[:].bitcast(FP8X4), lhsT_scale=q_scales[:],
+                            rhs=fw_g[:].bitcast(FP8X4), rhs_scale=fs_g[:], start=False, stop=True)
+
+        v_bf = [sb.tile([P, HALF, 4], BF16, name="v_bf%d" % h, align_bytes=64) for h in range(2)]
+        v_codes = [sb.tile([P, HALF], U32, name="v_codes%d" % h, align_bytes=64) for h in range(2)]
+        v_scales = [sb.tile([P, HALF], U8, name="v_scales%d" % h, align_bytes=64) for h in range(2)]
+
+        def weave(engine_copy, h, c):
+            cols = slice(c * QUART, (c + 1) * QUART)
+            engine_copy(v_bf[h][:, cols, :], v_raw[h][:, :, cols].rearrange("p j e -> p e j"))
+
+        def quantize_vals(h):
+            nc.vector.quantize_mx(out=v_codes[h][:].bitcast(FP8X4), scales=v_scales[h][:],
+                                  in_=v_bf[h][:].rearrange("p e j -> p (e j)"))
+
+        weave(nc.scalar.copy, 0, 0)
+        neg_max = sb.tile([P, 1], F32, name="neg_max")
+        nc.vector.tensor_reduce(neg_max[:], scores[:], mybir.AxisListType.X, ALU.max, negate=True)
+        prob = sb.tile([P, 2, P, 2], F32, name="prob")
+        row_sum = sb.tile([P, 1], F32, name="row_sum")
+        nc.scalar.activation(prob[:], scores[:].rearrange("p (s u e) -> p u s e", u=2, e=2), ACT.Exp,
+                             bias=neg_max[:], accum_out=row_sum[:])
+        weave(nc.vector.tensor_copy, 0, 1)
+        quantize_vals(0)
+        inv_sum = sb.tile([P, 1], F32, name="inv_sum")
+        nc.vector.reciprocal(inv_sum[:], row_sum[:])
+        w_bf = sb.tile([P, 2, P, 2], BF16, name="w_bf", align_bytes=64)
+        wt_ps = ps.tile([P, 2, Q], F32, name="wt_ps")
+        for u in range(2):
+            nc.vector.scalar_tensor_tensor(w_bf[:, u, :, :], prob[:, u, :, :], inv_sum[:],
+                                           size_ps[:, :, u, :].rearrange("p e s -> p s e"), ALU.mult, ALU.mult)
+            nc.tensor.transpose(wt_ps[:, u, :], w_bf[:, u, :, :].rearrange("p s e -> p (s e)").bitcast(F32), ident[:])
+        weave(nc.scalar.copy, 1, 0)
+        weave(nc.vector.tensor_copy, 1, 1)
+        quantize_vals(1)
+        wt_bf = sb.tile([P, Q, 4], BF16, name="wt_bf", align_bytes=64)
+        nc.scalar.copy(wt_bf[:].rearrange("p q j -> p (q j)").bitcast(F32).rearrange("p (q u) -> p q u", u=2),
+                       wt_ps[:].rearrange("p u q -> p q u"))
+        w_codes = sb.tile([P, Q], U32, name="w_codes", align_bytes=64)
+        w_scales = sb.tile([P, Q], U8, name="w_scales", align_bytes=64)
+        nc.vector.quantize_mx(out=w_codes[:].bitcast(FP8X4), scales=w_scales[:], in_=wt_bf[:].rearrange("p q j -> p (q j)"))
+
+        for h, (engine_copy, queue) in enumerate(((nc.vector.tensor_copy, nc.sync), (nc.scalar.copy, nc.scalar))):
+            acc = ps.tile([P, HALF], F32, name="acc%d" % h)
+            nc.tensor.matmul_mx(out=acc[:], lhsT=w_codes[:].bitcast(FP8X4), lhsT_scale=w_scales[:],
+                                rhs=v_codes[h][:].bitcast(FP8X4), rhs_scale=v_scales[h][:], start=True, stop=True)
+            res = sb.tile([P, HALF], F32, name="res%d" % h, align_bytes=64)
+            engine_copy(res[:], acc[:])
+            queue.dma_start(out[:, h * HALF:(h + 1) * HALF], res[:])

@@ -17,7 +17,9 @@ ALU = mybir.AluOpType
 ACT = mybir.ActivationFunctionType
 P = 128
 HALF = E // 2
-QUART = E // 4
+FIRST = 192
+SLOTS = I // 2
+LIST_COLS = SLOTS // 16
 
 
 def tile_attend_pqresid_kernel(tc, query, book_words, book_scales, fine_words, fine_scales, size, vals, offs, offs2, out):
@@ -29,48 +31,44 @@ def tile_attend_pqresid_kernel(tc, query, book_words, book_scales, fine_words, f
         book_list = sb.tile([P, I // 16], U16, name="book_list")
         fine_list = sb.tile([P, I // 16], U16, name="fine_list")
         bs_win = sb.tile([P, C], U8, name="bs_win", align_bytes=64)
-        fs_win = sb.tile([P, T], U8, name="fs_win", tag="first", align_bytes=64)
-        bw_win = sb.tile([P, C], I32, name="bw_win", tag="second", align_bytes=64)
+        fs_win = sb.tile([P, T], U8, name="fs_win", tag="late", align_bytes=64)
+        bw_win = sb.tile([P, C], I32, name="bw_win", tag="early", align_bytes=64)
         fw_win = sb.tile([P, T], I32, name="fw_win", align_bytes=64)
-        q_raw = sb.tile([P, 4, Q], F32, name="q_raw", align_bytes=64)
+        q_raw = sb.tile([P, 4, Q], F32, name="q_raw", tag="after_query", align_bytes=64)
         size_col = sb.tile([P, 4], F32, name="size_col")
 
-        nc.vector.memset(bs_win[:].bitcast(I32), 0)
         nc.vector.memset(fs_win[:].bitcast(I32), 0)
         nc.sync.dma_start(book_list[:], offs)
-        nc.sync.dma_start(fine_list[:], offs2)
-        for w in range(2):
-            nc.scalar.dma_start(bs_win[w:P:16, :].bitcast(I32), book_scales[0, w:16:2, :].bitcast(I32))
+        nc.scalar.dma_start(size_col[:], size.rearrange("o (s t) -> (o s) t", t=4))
+        nc.sync.dma_start(bs_win[:].bitcast(I32), book_scales[0].bitcast(I32).unsqueeze(1).to_broadcast([16, 8, C // 4]))
         nc.sync.dma_start(bw_win[:], book_words[0].rearrange("p c t -> p (c t)").bitcast(I32))
+        for v in range(4):
+            nc.scalar.dma_start(fs_win[v:P:32, :].bitcast(I32), fine_scales[0, v:16:4, :].bitcast(I32))
+        nc.sync.dma_start(fine_list[:], offs2)
         nc.sync.dma_start(q_raw[:], query.rearrange("(p j) q -> p j q", j=4))
         nc.sync.dma_start(fw_win[:], fine_words[0].rearrange("p c t -> p (c t)").bitcast(I32))
-        for x, queue in enumerate((nc.scalar, nc.scalar, nc.gpsimd, nc.gpsimd)):
-            queue.dma_start(fs_win[32 * x:32 * x + 4, :].bitcast(I32), fine_scales[0, 4 * x:4 * x + 4, :].bitcast(I32))
-        nc.sync.dma_start(size_col[:], size.rearrange("o (s t) -> (o s) t", t=4))
 
-        ident = sb.tile([P, P], F32, name="ident")
-        make_identity(nc, ident[:])
-        bs_pl = sb.tile([P, I], U8, name="bs_pl", align_bytes=64)
         warm = sb.tile([P, 1], F32, name="warm")
         nc.vector.memset(warm[:], 0.0)
         warm_out = sb.tile([P, 1], F32, name="warm_out")
         nc.scalar.activation(warm_out[:], warm[:], ACT.Exp)
+        ident = sb.tile([P, P], F32, name="ident")
+        make_identity(nc, ident[:])
+        bs_pl = sb.tile([P, I], U8, name="bs_pl", align_bytes=64)
+        nc.gpsimd.memset(bs_pl[:].bitcast(I32), 0)
 
         bs_g = sb.tile([P, I], U8, name="bs_g", align_bytes=64)
         fs_g = sb.tile([P, I], U8, name="fs_g", align_bytes=64)
         bw_g = sb.tile([P, I], I32, name="bw_g", align_bytes=64)
         fw_g = sb.tile([P, I], I32, name="fw_g", align_bytes=64)
         nc.vector.tensor_copy(bs_g[:], bs_win[:].indirect(book_list[:]))
-        nc.vector.tensor_copy(bs_pl[:].bitcast(I32), bs_g[:].bitcast(I32))
-        for w in range(2):
-            nc.scalar.dma_start(bs_pl[2 + w:P:32, :].bitcast(I32), bs_g[16 + w:P:32, :].bitcast(I32))
+        for x in range(4):
+            nc.scalar.dma_start(bs_pl[32 * x:32 * x + 4, :].bitcast(I32), bs_g[32 * x:32 * x + 32:8, :].bitcast(I32))
         nc.vector.tensor_copy(bw_g[:].bitcast(U32), bw_win[:].bitcast(U32).indirect(book_list[:]))
         nc.vector.tensor_copy(fs_g[:], fs_win[:].indirect(fine_list[:]))
         vals_rows = vals.rearrange("(p j) e -> p j e", j=4)
-        v_raw = []
-        for h, tag in enumerate(("second", "first")):
-            v_raw.append(sb.tile([P, 4, HALF], F32, name="v_raw%d" % h, tag=tag, align_bytes=64))
-            nc.sync.dma_start(v_raw[h][:], vals_rows[:, :, h * HALF:(h + 1) * HALF])
+        v_first = sb.tile([P, 4, FIRST], F32, name="v_first", tag="early", align_bytes=64)
+        nc.sync.dma_start(v_first[:], vals_rows[:, :, 0:FIRST])
 
         size_ps = ps.tile([P, 2, 2, P], F32, name="size_ps")
         for u in range(2):
@@ -80,50 +78,63 @@ def tile_attend_pqresid_kernel(tc, query, book_words, book_scales, fine_words, f
 
         q_bf = sb.tile([P, Q, 4], BF16, name="q_bf", align_bytes=64)
         nc.scalar.copy(q_bf[:], q_raw[:].rearrange("p j q -> p q j"))
+        v_rest = sb.tile([P, 4, E - FIRST], F32, name="v_rest", tag="after_query", align_bytes=64)
+        nc.sync.dma_start(v_rest[:], vals_rows[:, :, FIRST:E])
         q_codes = sb.tile([P, Q], U32, name="q_codes", align_bytes=64)
-        q_scales = sb.tile([P, Q], U8, name="q_scales", align_bytes=64)
+        q_scales = sb.tile([P, Q], U8, name="q_scales", tag="late", align_bytes=64)
         nc.vector.quantize_mx(out=q_codes[:].bitcast(FP8X4), scales=q_scales[:], in_=q_bf[:].rearrange("p q j -> p (q j)"))
 
-        nc.vector.tensor_copy(fw_g[:].bitcast(U32), fw_win[:].bitcast(U32).indirect(fine_list[:]))
+        scores = [ps.tile([P, SLOTS], F32, name="scores%d" % h) for h in range(2)]
+        for h in range(2):
+            cols = slice(h * SLOTS, (h + 1) * SLOTS)
+            nc.tensor.matmul_mx(out=scores[h][:], lhsT=q_codes[:].bitcast(FP8X4), lhsT_scale=q_scales[:],
+                                rhs=bw_g[:, cols].bitcast(FP8X4), rhs_scale=bs_pl[:, cols], start=True, stop=False)
+        for h in range(2):
+            cols = slice(h * SLOTS, (h + 1) * SLOTS)
+            nc.vector.tensor_copy(fw_g[:, cols].bitcast(U32),
+                                  fw_win[:].bitcast(U32).indirect(fine_list[:, h * LIST_COLS:(h + 1) * LIST_COLS]))
+            nc.tensor.matmul_mx(out=scores[h][:], lhsT=q_codes[:].bitcast(FP8X4), lhsT_scale=q_scales[:],
+                                rhs=fw_g[:, cols].bitcast(FP8X4), rhs_scale=fs_g[:, cols], start=False, stop=True)
 
-        scores = ps.tile([P, I], F32, name="scores")
-        nc.tensor.matmul_mx(out=scores[:], lhsT=q_codes[:].bitcast(FP8X4), lhsT_scale=q_scales[:],
-                            rhs=bw_g[:].bitcast(FP8X4), rhs_scale=bs_pl[:], start=True, stop=False)
-        nc.tensor.matmul_mx(out=scores[:], lhsT=q_codes[:].bitcast(FP8X4), lhsT_scale=q_scales[:],
-                            rhs=fw_g[:].bitcast(FP8X4), rhs_scale=fs_g[:], start=False, stop=True)
-
-        v_bf = [sb.tile([P, HALF, 4], BF16, name="v_bf%d" % h, align_bytes=64) for h in range(2)]
-        v_codes = [sb.tile([P, HALF], U32, name="v_codes%d" % h, align_bytes=64) for h in range(2)]
-        v_scales = [sb.tile([P, HALF], U8, name="v_scales%d" % h, align_bytes=64) for h in range(2)]
-
-        def weave(engine_copy, h, c):
-            cols = slice(c * QUART, (c + 1) * QUART)
-            engine_copy(v_bf[h][:, cols, :], v_raw[h][:, :, cols].rearrange("p j e -> p e j"))
-
-        def quantize_vals(h):
-            nc.vector.quantize_mx(out=v_codes[h][:].bitcast(FP8X4), scales=v_scales[h][:],
-                                  in_=v_bf[h][:].rearrange("p e j -> p (e j)"))
-
-        weave(nc.scalar.copy, 0, 0)
+        neg_max0 = sb.tile([P, 1], F32, name="neg_max0")
         neg_max = sb.tile([P, 1], F32, name="neg_max")
-        nc.vector.tensor_reduce(neg_max[:], scores[:], mybir.AxisListType.X, ALU.max, negate=True)
-        prob = sb.tile([P, 2, P, 2], F32, name="prob")
+        neg_scores1 = sb.tile([P, SLOTS], F32, name="neg_scores1", tag="after_exp", align_bytes=64)
+        nc.vector.tensor_reduce(neg_max0[:], scores[0][:], mybir.AxisListType.X, ALU.max, negate=True)
+        nc.vector.tensor_scalar(neg_scores1[:], scores[1][:], -1.0, neg_max0[:], ALU.mult, ALU.min, accum_out=neg_max[:])
+
+        v_bf0 = sb.tile([P, HALF, 4], BF16, name="v_bf0", align_bytes=64)
+        nc.scalar.copy(v_bf0[:, 0:FIRST, :], v_first[:].rearrange("p j e -> p e j"))
+        prob = [sb.tile([P, 2, P // 2, 2], F32, name="prob%d" % h) for h in range(2)]
+        sized = sb.tile([P, 2, P, 2], F32, name="sized", tag="after_weights", align_bytes=64)
+        sums = [sb.tile([P, 1], F32, name="sum%d" % h) for h in range(2)]
+        nc.scalar.activation(prob[0][:], scores[0][:].rearrange("p (s u e) -> p u s e", u=2, e=2), ACT.Exp,
+                             bias=neg_max[:], accum_out=sums[0][:])
+        nc.scalar.activation(prob[1][:], neg_scores1[:].rearrange("p (s u e) -> p u s e", u=2, e=2), ACT.Exp,
+                             bias=neg_max[:], scale=-1.0, accum_out=sums[1][:])
+        nc.vector.tensor_tensor(sized[:, :, 0:64, :], prob[0][:],
+                                size_ps[:, :, :, 0:64].rearrange("p e u s -> p u s e"), ALU.mult)
         row_sum = sb.tile([P, 1], F32, name="row_sum")
-        nc.scalar.activation(prob[:], scores[:].rearrange("p (s u e) -> p u s e", u=2, e=2), ACT.Exp,
-                             bias=neg_max[:], accum_out=row_sum[:])
-        weave(nc.vector.tensor_copy, 0, 1)
-        quantize_vals(0)
         inv_sum = sb.tile([P, 1], F32, name="inv_sum")
+        nc.vector.tensor_tensor(row_sum[:], sums[0][:], sums[1][:], ALU.add)
+        nc.vector.tensor_tensor(sized[:, :, 64:128, :], prob[1][:],
+                                size_ps[:, :, :, 64:128].rearrange("p e u s -> p u s e"), ALU.mult)
+
         nc.vector.reciprocal(inv_sum[:], row_sum[:])
         w_bf = sb.tile([P, 2, P, 2], BF16, name="w_bf", align_bytes=64)
         wt_ps = ps.tile([P, 2, Q], F32, name="wt_ps")
         for u in range(2):
-            nc.vector.scalar_tensor_tensor(w_bf[:, u, :, :], prob[:, u, :, :], inv_sum[:],
-                                           size_ps[:, :, u, :].rearrange("p e s -> p s e"), ALU.mult, ALU.mult)
+            nc.vector.tensor_scalar(w_bf[:, u, :, :], sized[:, u, :, :], inv_sum[:], None, ALU.mult)
             nc.tensor.transpose(wt_ps[:, u, :], w_bf[:, u, :, :].rearrange("p s e -> p (s e)").bitcast(F32), ident[:])
-        weave(nc.scalar.copy, 1, 0)
-        weave(nc.vector.tensor_copy, 1, 1)
-        quantize_vals(1)
+
+        v_codes = [sb.tile([P, HALF], U32, name="v_codes0", tag="after_weights", align_bytes=64),
+                   sb.tile([P, HALF], U32, name="v_codes1", align_bytes=64)]
+        v_scales = [sb.tile([P, HALF], U8, name="v_scales%d" % h, align_bytes=64) for h in range(2)]
+        nc.vector.tensor_copy(v_bf0[:, FIRST:HALF, :], v_rest[:, :, 0:HALF - FIRST].rearrange("p j e -> p e j"))
+        v_bf1 = sb.tile([P, HALF, 4], BF16, name="v_bf1", tag="after_exp", align_bytes=64)
+        nc.scalar.copy(v_bf1[:], v_rest[:, :, HALF - FIRST:E - FIRST].rearrange("p j e -> p e j"))
+        for h, v_bf in enumerate((v_bf0, v_bf1)):
+            nc.vector.quantize_mx(out=v_codes[h][:].bitcast(FP8X4), scales=v_scales[h][:],
+                                  in_=v_bf[:].rearrange("p e j -> p (e j)"))
         wt_bf = sb.tile([P, Q, 4], BF16, name="wt_bf", align_bytes=64)
         nc.scalar.copy(wt_bf[:].rearrange("p q j -> p (q j)").bitcast(F32).rearrange("p (q u) -> p q u", u=2),
                        wt_ps[:].rearrange("p u q -> p q u"))

@@ -20,6 +20,7 @@ HALF = E // 2
 FIRST = 192
 SLOTS = I // 2
 LIST_COLS = SLOTS // 16
+PIECE = 128
 
 
 def tile_attend_pqresid_kernel(tc, query, book_words, book_scales, fine_words, fine_scales, size, vals, offs, offs2, out):
@@ -44,14 +45,10 @@ def tile_attend_pqresid_kernel(tc, query, book_words, book_scales, fine_words, f
         nc.sync.dma_start(bw_win[:], book_words[0].rearrange("p c t -> p (c t)").bitcast(I32))
         for v in range(4):
             nc.scalar.dma_start(fs_win[v:P:32, :].bitcast(I32), fine_scales[0, v:16:4, :].bitcast(I32))
-        nc.sync.dma_start(fine_list[:], offs2)
         nc.sync.dma_start(q_raw[:], query.rearrange("(p j) q -> p j q", j=4))
+        nc.sync.dma_start(fine_list[:], offs2)
         nc.sync.dma_start(fw_win[:], fine_words[0].rearrange("p c t -> p (c t)").bitcast(I32))
 
-        warm = sb.tile([P, 1], F32, name="warm")
-        nc.vector.memset(warm[:], 0.0)
-        warm_out = sb.tile([P, 1], F32, name="warm_out")
-        nc.scalar.activation(warm_out[:], warm[:], ACT.Exp)
         ident = sb.tile([P, P], F32, name="ident")
         make_identity(nc, ident[:])
         bs_pl = sb.tile([P, I], U8, name="bs_pl", align_bytes=64)
@@ -63,7 +60,7 @@ def tile_attend_pqresid_kernel(tc, query, book_words, book_scales, fine_words, f
         fw_g = sb.tile([P, I], I32, name="fw_g", align_bytes=64)
         nc.vector.tensor_copy(bs_g[:], bs_win[:].indirect(book_list[:]))
         for x in range(4):
-            nc.scalar.dma_start(bs_pl[32 * x:32 * x + 4, :].bitcast(I32), bs_g[32 * x:32 * x + 32:8, :].bitcast(I32))
+            nc.sync.dma_start(bs_pl[32 * x:32 * x + 4, :].bitcast(I32), bs_g[32 * x:32 * x + 32:8, :].bitcast(I32))
         nc.vector.tensor_copy(bw_g[:].bitcast(U32), bw_win[:].bitcast(U32).indirect(book_list[:]))
         nc.vector.tensor_copy(fs_g[:], fs_win[:].indirect(fine_list[:]))
         vals_rows = vals.rearrange("(p j) e -> p j e", j=4)
@@ -77,7 +74,7 @@ def tile_attend_pqresid_kernel(tc, query, book_words, book_scales, fine_words, f
                 nc.tensor.transpose(size_ps[:, e, u, :], size_col[:, t:t + 1].to_broadcast([P, P]), ident[:])
 
         q_bf = sb.tile([P, Q, 4], BF16, name="q_bf", align_bytes=64)
-        nc.scalar.copy(q_bf[:], q_raw[:].rearrange("p j q -> p q j"))
+        nc.scalar.activation(q_bf[:].rearrange("p (c i) j -> p c j i", i=4), q_raw[:].rearrange("p j (c i) -> p c j i", i=4), ACT.Copy)
         v_rest = sb.tile([P, 4, E - FIRST], F32, name="v_rest", tag="after_query", align_bytes=64)
         nc.sync.dma_start(v_rest[:], vals_rows[:, :, FIRST:E])
         q_codes = sb.tile([P, Q], U32, name="q_codes", align_bytes=64)
@@ -89,8 +86,6 @@ def tile_attend_pqresid_kernel(tc, query, book_words, book_scales, fine_words, f
             cols = slice(h * SLOTS, (h + 1) * SLOTS)
             nc.tensor.matmul_mx(out=scores[h][:], lhsT=q_codes[:].bitcast(FP8X4), lhsT_scale=q_scales[:],
                                 rhs=bw_g[:, cols].bitcast(FP8X4), rhs_scale=bs_pl[:, cols], start=True, stop=False)
-        for h in range(2):
-            cols = slice(h * SLOTS, (h + 1) * SLOTS)
             nc.vector.tensor_copy(fw_g[:, cols].bitcast(U32),
                                   fw_win[:].bitcast(U32).indirect(fine_list[:, h * LIST_COLS:(h + 1) * LIST_COLS]))
             nc.tensor.matmul_mx(out=scores[h][:], lhsT=q_codes[:].bitcast(FP8X4), lhsT_scale=q_scales[:],
@@ -98,40 +93,32 @@ def tile_attend_pqresid_kernel(tc, query, book_words, book_scales, fine_words, f
 
         neg_max0 = sb.tile([P, 1], F32, name="neg_max0")
         neg_max = sb.tile([P, 1], F32, name="neg_max")
-        neg_scores1 = sb.tile([P, SLOTS], F32, name="neg_scores1", tag="after_exp", align_bytes=64)
-        nc.vector.tensor_reduce(neg_max0[:], scores[0][:], mybir.AxisListType.X, ALU.max, negate=True)
-        nc.vector.tensor_scalar(neg_scores1[:], scores[1][:], -1.0, neg_max0[:], ALU.mult, ALU.min, accum_out=neg_max[:])
+        neg_scores = sb.tile([P, 2, P, 2], F32, name="neg_scores", tag="after_exp", align_bytes=64)
+        for h, (start, found) in enumerate(((None, neg_max0[:]), (neg_max0[:], neg_max[:]))):
+            nc.vector.tensor_scalar(neg_scores[:, :, h * 64:(h + 1) * 64, :],
+                                    scores[h][:].rearrange("p (s u e) -> p u s e", u=2, e=2),
+                                    -1.0, start, ALU.mult, ALU.min, accum_out=found)
 
         v_bf0 = sb.tile([P, HALF, 4], BF16, name="v_bf0", align_bytes=64)
-        nc.scalar.copy(v_bf0[:, 0:FIRST, :], v_first[:].rearrange("p j e -> p e j"))
-        prob = [sb.tile([P, 2, P // 2, 2], F32, name="prob%d" % h) for h in range(2)]
-        sized = sb.tile([P, 2, P, 2], F32, name="sized", tag="after_weights", align_bytes=64)
-        sums = [sb.tile([P, 1], F32, name="sum%d" % h) for h in range(2)]
-        nc.scalar.activation(prob[0][:], scores[0][:].rearrange("p (s u e) -> p u s e", u=2, e=2), ACT.Exp,
-                             bias=neg_max[:], accum_out=sums[0][:])
-        nc.scalar.activation(prob[1][:], neg_scores1[:].rearrange("p (s u e) -> p u s e", u=2, e=2), ACT.Exp,
-                             bias=neg_max[:], scale=-1.0, accum_out=sums[1][:])
-        nc.vector.tensor_tensor(sized[:, :, 0:64, :], prob[0][:],
-                                size_ps[:, :, :, 0:64].rearrange("p e u s -> p u s e"), ALU.mult)
+        nc.scalar.copy(v_bf0[:, 0:FIRST, :].rearrange("p (c i) j -> p c j i", i=4), v_first[:].rearrange("p j (c i) -> p c j i", i=4))
+        prob = sb.tile([P, 2, P, 2], F32, name="prob", tag="early", align_bytes=64)
         row_sum = sb.tile([P, 1], F32, name="row_sum")
+        nc.scalar.activation(prob[:], neg_scores[:], ACT.Exp, bias=neg_max[:], scale=-1.0, accum_out=row_sum[:])
         inv_sum = sb.tile([P, 1], F32, name="inv_sum")
-        nc.vector.tensor_tensor(row_sum[:], sums[0][:], sums[1][:], ALU.add)
-        nc.vector.tensor_tensor(sized[:, :, 64:128, :], prob[1][:],
-                                size_ps[:, :, :, 64:128].rearrange("p e u s -> p u s e"), ALU.mult)
-
         nc.vector.reciprocal(inv_sum[:], row_sum[:])
         w_bf = sb.tile([P, 2, P, 2], BF16, name="w_bf", align_bytes=64)
         wt_ps = ps.tile([P, 2, Q], F32, name="wt_ps")
         for u in range(2):
-            nc.vector.tensor_scalar(w_bf[:, u, :, :], sized[:, u, :, :], inv_sum[:], None, ALU.mult)
+            nc.vector.scalar_tensor_tensor(w_bf[:, u, :, :], prob[:, u, :, :], inv_sum[:],
+                                           size_ps[:, :, u, :].rearrange("p e s -> p s e"), ALU.mult, ALU.mult)
             nc.tensor.transpose(wt_ps[:, u, :], w_bf[:, u, :, :].rearrange("p s e -> p (s e)").bitcast(F32), ident[:])
 
-        v_codes = [sb.tile([P, HALF], U32, name="v_codes0", tag="after_weights", align_bytes=64),
+        v_codes = [sb.tile([P, HALF], U32, name="v_codes0", tag="early", align_bytes=64),
                    sb.tile([P, HALF], U32, name="v_codes1", align_bytes=64)]
         v_scales = [sb.tile([P, HALF], U8, name="v_scales%d" % h, align_bytes=64) for h in range(2)]
-        nc.vector.tensor_copy(v_bf0[:, FIRST:HALF, :], v_rest[:, :, 0:HALF - FIRST].rearrange("p j e -> p e j"))
+        nc.scalar.copy(v_bf0[:, FIRST:HALF, :].rearrange("p (c i) j -> p c j i", i=4), v_rest[:, :, 0:HALF - FIRST].rearrange("p j (c i) -> p c j i", i=4))
         v_bf1 = sb.tile([P, HALF, 4], BF16, name="v_bf1", tag="after_exp", align_bytes=64)
-        nc.scalar.copy(v_bf1[:], v_rest[:, :, HALF - FIRST:E - FIRST].rearrange("p j e -> p e j"))
+        nc.scalar.copy(v_bf1[:].rearrange("p (c i) j -> p c j i", i=4), v_rest[:, :, HALF - FIRST:E - FIRST].rearrange("p j (c i) -> p c j i", i=4))
         for h, v_bf in enumerate((v_bf0, v_bf1)):
             nc.vector.quantize_mx(out=v_codes[h][:].bitcast(FP8X4), scales=v_scales[h][:],
                                   in_=v_bf[:].rearrange("p e j -> p (e j)"))
@@ -142,10 +129,14 @@ def tile_attend_pqresid_kernel(tc, query, book_words, book_scales, fine_words, f
         w_scales = sb.tile([P, Q], U8, name="w_scales", align_bytes=64)
         nc.vector.quantize_mx(out=w_codes[:].bitcast(FP8X4), scales=w_scales[:], in_=wt_bf[:].rearrange("p q j -> p (q j)"))
 
-        for h, (engine_copy, queue) in enumerate(((nc.vector.tensor_copy, nc.sync), (nc.scalar.copy, nc.scalar))):
-            acc = ps.tile([P, HALF], F32, name="acc%d" % h)
-            nc.tensor.matmul_mx(out=acc[:], lhsT=w_codes[:].bitcast(FP8X4), lhsT_scale=w_scales[:],
-                                rhs=v_codes[h][:].bitcast(FP8X4), rhs_scale=v_scales[h][:], start=True, stop=True)
+        turn = 0
+        for h, queue in enumerate((nc.sync, nc.scalar)):
             res = sb.tile([P, HALF], F32, name="res%d" % h, align_bytes=64)
-            engine_copy(res[:], acc[:])
+            for c in range(HALF // PIECE):
+                cols = slice(c * PIECE, (c + 1) * PIECE)
+                acc = ps.tile([P, PIECE], F32, name="acc%d" % turn)
+                nc.tensor.matmul_mx(out=acc[:], lhsT=w_codes[:].bitcast(FP8X4), lhsT_scale=w_scales[:],
+                                    rhs=v_codes[h][:, cols].bitcast(FP8X4), rhs_scale=v_scales[h][:, cols], start=True, stop=True)
+                (nc.vector.tensor_copy, nc.scalar.copy)[turn % 2](res[:, cols], acc[:])
+                turn = turn + 1
             queue.dma_start(out[:, h * HALF:(h + 1) * HALF], res[:])

@@ -38,10 +38,11 @@ def tile_attend_pqresid_kernel(tc, query, book_words, book_scales, fine_words, f
         q_raw = sb.tile([P, 4, Q], F32, name="q_raw", tag="after_query", align_bytes=64)
         size_col = sb.tile([P, 4], F32, name="size_col")
 
+        nc.gpsimd.memset(bs_win[:].bitcast(I32), 0)
         nc.vector.memset(fs_win[:].bitcast(I32), 0)
         nc.sync.dma_start(book_list[:], offs)
         nc.scalar.dma_start(size_col[:], size.rearrange("o (s t) -> (o s) t", t=4))
-        nc.sync.dma_start(bs_win[:].bitcast(I32), book_scales[0].bitcast(I32).unsqueeze(1).to_broadcast([16, 8, C // 4]))
+        nc.sync.dma_start(bs_win[0:P:8, :].bitcast(I32), book_scales[0].bitcast(I32))
         nc.sync.dma_start(bw_win[:], book_words[0].rearrange("p c t -> p (c t)").bitcast(I32))
         for v in range(4):
             nc.scalar.dma_start(fs_win[v:P:32, :].bitcast(I32), fine_scales[0, v:16:4, :].bitcast(I32))

@@ -17,7 +17,9 @@ ALU = mybir.AluOpType
 ACT = mybir.ActivationFunctionType
 P = 128
 HALF = E // 2
-FIRST = 192
+FIRST = 256
+ON_SCALAR = 192
+KEYS_AT = 16 * E
 SLOTS = I // 2
 LIST_COLS = SLOTS // 16
 PIECE = 128
@@ -27,45 +29,47 @@ def tile_attend_pqresid_kernel(tc, query, book_words, book_scales, fine_words, f
     nc = tc.nc
     with ExitStack() as ctx:
         sb = ctx.enter_context(tc.tile_pool(name="sb", bufs=1))
+        shared = ctx.enter_context(tc.tile_pool(name="shared", bufs=1))
         ps = ctx.enter_context(tc.psum_pool(name="ps", bufs=1))
 
         book_list = sb.tile([P, I // 16], U16, name="book_list")
         fine_list = sb.tile([P, I // 16], U16, name="fine_list")
-        bs_win = sb.tile([P, C], U8, name="bs_win", align_bytes=64)
-        fs_win = sb.tile([P, T], U8, name="fs_win", tag="late", align_bytes=64)
-        bw_win = sb.tile([P, C], I32, name="bw_win", tag="early", align_bytes=64)
+        bs_win = shared.tile([P, C], U8, name="bs_win", align_bytes=64, offset=16 * FIRST - C // 2)
+        fs_win = sb.tile([P, T], U8, name="fs_win", align_bytes=64)
+        bw_win = sb.tile([P, C], I32, name="bw_win", align_bytes=64)
         fw_win = sb.tile([P, T], I32, name="fw_win", align_bytes=64)
-        q_raw = sb.tile([P, 4, Q], F32, name="q_raw", tag="after_query", align_bytes=64)
+        q_raw = sb.tile([P, 4, Q], F32, name="q_raw", align_bytes=64)
         size_col = sb.tile([P, 4], F32, name="size_col")
 
-        nc.gpsimd.memset(bs_win[:].bitcast(I32), 0)
+        nc.vector.memset(bs_win[:].bitcast(I32), 0)
         nc.vector.memset(fs_win[:].bitcast(I32), 0)
         nc.sync.dma_start(book_list[:], offs)
         nc.scalar.dma_start(size_col[:], size.rearrange("o (s t) -> (o s) t", t=4))
+        nc.sync.dma_start(fine_list[:], offs2)
         nc.sync.dma_start(bs_win[0:P:8, :].bitcast(I32), book_scales[0].bitcast(I32))
         nc.sync.dma_start(bw_win[:], book_words[0].rearrange("p c t -> p (c t)").bitcast(I32))
-        for v in range(4):
-            nc.scalar.dma_start(fs_win[v:P:32, :].bitcast(I32), fine_scales[0, v:16:4, :].bitcast(I32))
         nc.sync.dma_start(q_raw[:], query.rearrange("(p j) q -> p j q", j=4))
-        nc.sync.dma_start(fine_list[:], offs2)
+        for v in range(4):
+            nc.sync.dma_start(fs_win[v:P:32, :].bitcast(I32), fine_scales[0, v:16:4, :].bitcast(I32))
         nc.sync.dma_start(fw_win[:], fine_words[0].rearrange("p c t -> p (c t)").bitcast(I32))
 
         ident = sb.tile([P, P], F32, name="ident")
-        make_identity(nc, ident[:])
         bs_pl = sb.tile([P, I], U8, name="bs_pl", align_bytes=64)
-        nc.gpsimd.memset(bs_pl[:].bitcast(I32), 0)
+        nc.vector.memset(bs_pl[:].bitcast(I32), 0)
+        nc.vector.memset(ident[:], 0.0)
+        make_identity(nc, ident[:], nomemset=True)
 
         bs_g = sb.tile([P, I], U8, name="bs_g", align_bytes=64)
         fs_g = sb.tile([P, I], U8, name="fs_g", align_bytes=64)
         bw_g = sb.tile([P, I], I32, name="bw_g", align_bytes=64)
-        fw_g = sb.tile([P, I], I32, name="fw_g", align_bytes=64)
+        fw_g = shared.tile([P, I], I32, name="fw_g", align_bytes=64, offset=KEYS_AT)
         nc.vector.tensor_copy(bs_g[:], bs_win[:].indirect(book_list[:]))
         for x in range(4):
             nc.sync.dma_start(bs_pl[32 * x:32 * x + 4, :].bitcast(I32), bs_g[32 * x:32 * x + 32:8, :].bitcast(I32))
         nc.vector.tensor_copy(bw_g[:].bitcast(U32), bw_win[:].bitcast(U32).indirect(book_list[:]))
         nc.vector.tensor_copy(fs_g[:], fs_win[:].indirect(fine_list[:]))
         vals_rows = vals.rearrange("(p j) e -> p j e", j=4)
-        v_first = sb.tile([P, 4, FIRST], F32, name="v_first", tag="early", align_bytes=64)
+        v_first = shared.tile([P, 4, FIRST], F32, name="v_first", align_bytes=64, offset=0)
         nc.sync.dma_start(v_first[:], vals_rows[:, :, 0:FIRST])
 
         size_ps = ps.tile([P, 2, 2, P], F32, name="size_ps")
@@ -76,10 +80,10 @@ def tile_attend_pqresid_kernel(tc, query, book_words, book_scales, fine_words, f
 
         q_bf = sb.tile([P, Q, 4], BF16, name="q_bf", align_bytes=64)
         nc.scalar.activation(q_bf[:].rearrange("p (c i) j -> p c j i", i=4), q_raw[:].rearrange("p j (c i) -> p c j i", i=4), ACT.Copy)
-        v_rest = sb.tile([P, 4, E - FIRST], F32, name="v_rest", tag="after_query", align_bytes=64)
+        v_rest = shared.tile([P, 4, E - FIRST], F32, name="v_rest", align_bytes=64, offset=16 * FIRST)
         nc.sync.dma_start(v_rest[:], vals_rows[:, :, FIRST:E])
         q_codes = sb.tile([P, Q], U32, name="q_codes", align_bytes=64)
-        q_scales = sb.tile([P, Q], U8, name="q_scales", tag="late", align_bytes=64)
+        q_scales = sb.tile([P, Q], U8, name="q_scales", align_bytes=64)
         nc.vector.quantize_mx(out=q_codes[:].bitcast(FP8X4), scales=q_scales[:], in_=q_bf[:].rearrange("p q j -> p (q j)"))
 
         scores = [ps.tile([P, SLOTS], F32, name="scores%d" % h) for h in range(2)]
@@ -100,9 +104,16 @@ def tile_attend_pqresid_kernel(tc, query, book_words, book_scales, fine_words, f
                                     scores[h][:].rearrange("p (s u e) -> p u s e", u=2, e=2),
                                     -1.0, start, ALU.mult, ALU.min, accum_out=found)
 
-        v_bf0 = sb.tile([P, HALF, 4], BF16, name="v_bf0", align_bytes=64)
-        nc.scalar.copy(v_bf0[:, 0:FIRST, :].rearrange("p (c i) j -> p c j i", i=4), v_first[:].rearrange("p j (c i) -> p c j i", i=4))
-        prob = sb.tile([P, 2, P, 2], F32, name="prob", tag="early", align_bytes=64)
+        v_bf0 = sb.tile([P, ON_SCALAR, 4], BF16, name="v_bf0", align_bytes=64)
+        nc.scalar.copy(v_bf0[:].rearrange("p (c i) j -> p c j i", i=4), v_first[:, :, 0:ON_SCALAR].rearrange("p j (c i) -> p c j i", i=4))
+        v_codes = [shared.tile([P, HALF], U32, name="v_codes0", align_bytes=64, offset=KEYS_AT),
+                   sb.tile([P, HALF], U32, name="v_codes1", align_bytes=64)]
+        v_scales = [sb.tile([P, HALF], U8, name="v_scales%d" % h, align_bytes=64) for h in range(2)]
+        v_bf2 = shared.tile([P, HALF - ON_SCALAR, 4], BF16, name="v_bf2", align_bytes=64, offset=KEYS_AT + 4 * HALF)
+        nc.vector.tensor_copy(v_bf2[:].rearrange("p (c i) j -> p c j i", i=4), v_first[:, :, ON_SCALAR:HALF].rearrange("p j (c i) -> p c j i", i=4))
+        for lo, hi, src in ((0, 128, v_bf0[:, 0:128, :]), (128, ON_SCALAR, v_bf0[:, 128:ON_SCALAR, :]), (ON_SCALAR, HALF, v_bf2[:])):
+            nc.vector.quantize_mx(out=v_codes[0][:, lo:hi].bitcast(FP8X4), scales=v_scales[0][:, lo:hi], in_=src.rearrange("p e j -> p (e j)"))
+        prob = sb.tile([P, 2, P, 2], F32, name="prob", align_bytes=64)
         row_sum = sb.tile([P, 1], F32, name="row_sum")
         nc.scalar.activation(prob[:], neg_scores[:], ACT.Exp, bias=neg_max[:], scale=-1.0, accum_out=row_sum[:])
         inv_sum = sb.tile([P, 1], F32, name="inv_sum")
@@ -114,15 +125,9 @@ def tile_attend_pqresid_kernel(tc, query, book_words, book_scales, fine_words, f
                                            size_ps[:, :, u, :].rearrange("p e s -> p s e"), ALU.mult, ALU.mult)
             nc.tensor.transpose(wt_ps[:, u, :], w_bf[:, u, :, :].rearrange("p s e -> p (s e)").bitcast(F32), ident[:])
 
-        v_codes = [sb.tile([P, HALF], U32, name="v_codes0", tag="early", align_bytes=64),
-                   sb.tile([P, HALF], U32, name="v_codes1", align_bytes=64)]
-        v_scales = [sb.tile([P, HALF], U8, name="v_scales%d" % h, align_bytes=64) for h in range(2)]
-        nc.scalar.copy(v_bf0[:, FIRST:HALF, :].rearrange("p (c i) j -> p c j i", i=4), v_rest[:, :, 0:HALF - FIRST].rearrange("p j (c i) -> p c j i", i=4))
         v_bf1 = sb.tile([P, HALF, 4], BF16, name="v_bf1", tag="after_exp", align_bytes=64)
-        nc.scalar.copy(v_bf1[:].rearrange("p (c i) j -> p c j i", i=4), v_rest[:, :, HALF - FIRST:E - FIRST].rearrange("p j (c i) -> p c j i", i=4))
-        for h, v_bf in enumerate((v_bf0, v_bf1)):
-            nc.vector.quantize_mx(out=v_codes[h][:].bitcast(FP8X4), scales=v_scales[h][:],
-                                  in_=v_bf[:].rearrange("p e j -> p (e j)"))
+        nc.scalar.copy(v_bf1[:].rearrange("p (c i) j -> p c j i", i=4), v_rest[:].rearrange("p j (c i) -> p c j i", i=4))
+        nc.vector.quantize_mx(out=v_codes[1][:].bitcast(FP8X4), scales=v_scales[1][:], in_=v_bf1[:].rearrange("p e j -> p (e j)"))
         wt_bf = sb.tile([P, Q, 4], BF16, name="wt_bf", align_bytes=64)
         nc.scalar.copy(wt_bf[:].rearrange("p q j -> p (q j)").bitcast(F32).rearrange("p (q u) -> p q u", u=2),
                        wt_ps[:].rearrange("p u q -> p q u"))

@@ -46,9 +46,9 @@ def tile_attend_pqresid_kernel(tc, query, book_words, book_scales, fine_words, f
         nc.sync.dma_start(book_list[:], offs)
         nc.scalar.dma_start(size_col[:], size.rearrange("o (s t) -> (o s) t", t=4))
         nc.sync.dma_start(fine_list[:], offs2)
+        nc.sync.dma_start(q_raw[:], query.rearrange("(p j) q -> p j q", j=4))
         nc.sync.dma_start(bs_win[0:P:8, :].bitcast(I32), book_scales[0].bitcast(I32))
         nc.sync.dma_start(bw_win[:], book_words[0].rearrange("p c t -> p (c t)").bitcast(I32))
-        nc.sync.dma_start(q_raw[:], query.rearrange("(p j) q -> p j q", j=4))
         for v in range(4):
             nc.sync.dma_start(fs_win[v:P:32, :].bitcast(I32), fine_scales[0, v:16:4, :].bitcast(I32))
         nc.sync.dma_start(fw_win[:], fine_words[0].rearrange("p c t -> p (c t)").bitcast(I32))

@@ -38,13 +38,11 @@ def tile_attend_pqresid_kernel(tc, query, book_words, book_scales, fine_words, f
         fs_win = sb.tile([P, T], U8, name="fs_win", align_bytes=64)
         bw_win = sb.tile([P, C], I32, name="bw_win", align_bytes=64)
         fw_win = sb.tile([P, T], I32, name="fw_win", align_bytes=64)
-        q_raw = sb.tile([P, 4, Q], F32, name="q_raw", align_bytes=64)
-        size_col = sb.tile([P, 4], F32, name="size_col")
+        q_raw = sb.tile([P, 4, Q], F32, name="q_raw", tag="query_then_size", align_bytes=64)
 
         nc.vector.memset(bs_win[:].bitcast(I32), 0)
         nc.vector.memset(fs_win[:].bitcast(I32), 0)
         nc.sync.dma_start(book_list[:], offs)
-        nc.scalar.dma_start(size_col[:], size.rearrange("o (s t) -> (o s) t", t=4))
         nc.sync.dma_start(fine_list[:], offs2)
         nc.sync.dma_start(q_raw[:], query.rearrange("(p j) q -> p j q", j=4))
         nc.sync.dma_start(bs_win[0:P:8, :].bitcast(I32), book_scales[0].bitcast(I32))
@@ -72,14 +70,16 @@ def tile_attend_pqresid_kernel(tc, query, book_words, book_scales, fine_words, f
         v_first = shared.tile([P, 4, FIRST], F32, name="v_first", align_bytes=64, offset=0)
         nc.sync.dma_start(v_first[:], vals_rows[:, :, 0:FIRST])
 
+        q_bf = sb.tile([P, Q, 4], BF16, name="q_bf", align_bytes=64)
+        nc.scalar.activation(q_bf[:].rearrange("p (c i) j -> p c j i", i=4), q_raw[:].rearrange("p j (c i) -> p c j i", i=4), ACT.Copy)
+        size_col = sb.tile([P, 4], F32, name="size_col", tag="query_then_size", align_bytes=64)
+        nc.scalar.dma_start(size_col[:], size.rearrange("o (s t) -> (o s) t", t=4))
         size_ps = ps.tile([P, 2, 2, P], F32, name="size_ps")
         for u in range(2):
             for e in range(2):
                 t = 2 * u + e
                 nc.tensor.transpose(size_ps[:, e, u, :], size_col[:, t:t + 1].to_broadcast([P, P]), ident[:])
 
-        q_bf = sb.tile([P, Q, 4], BF16, name="q_bf", align_bytes=64)
-        nc.scalar.activation(q_bf[:].rearrange("p (c i) j -> p c j i", i=4), q_raw[:].rearrange("p j (c i) -> p c j i", i=4), ACT.Copy)
         v_rest = shared.tile([P, 4, E - FIRST], F32, name="v_rest", align_bytes=64, offset=16 * FIRST)
         nc.sync.dma_start(v_rest[:], vals_rows[:, :, FIRST:E])
         q_codes = sb.tile([P, Q], U32, name="q_codes", align_bytes=64)

@@ -18,8 +18,8 @@ ACT = mybir.ActivationFunctionType
 P = 128
 HALF = E // 2
 FIRST = 256
-ON_SCALAR = 192
-KEYS_AT = 16 * E
+ON_SCALAR = 128
+KEYS_AT = 16 * E + 64
 SLOTS = I // 2
 LIST_COLS = SLOTS // 16
 PIECE = 128
@@ -38,13 +38,13 @@ def tile_attend_pqresid_kernel(tc, query, book_words, book_scales, fine_words, f
         fs_win = sb.tile([P, T], U8, name="fs_win", align_bytes=64)
         bw_win = sb.tile([P, C], I32, name="bw_win", align_bytes=64)
         fw_win = sb.tile([P, T], I32, name="fw_win", align_bytes=64)
-        q_raw = sb.tile([P, 4, Q], F32, name="q_raw", tag="query_then_size", align_bytes=64)
+        q_raw = sb.tile([P, 4, Q], F32, name="q_raw", align_bytes=64)
 
         nc.vector.memset(bs_win[:].bitcast(I32), 0)
         nc.vector.memset(fs_win[:].bitcast(I32), 0)
+        nc.sync.dma_start(q_raw[:], query.rearrange("(p j) q -> p j q", j=4))
         nc.sync.dma_start(book_list[:], offs)
         nc.sync.dma_start(fine_list[:], offs2)
-        nc.sync.dma_start(q_raw[:], query.rearrange("(p j) q -> p j q", j=4))
         nc.sync.dma_start(bs_win[0:P:8, :].bitcast(I32), book_scales[0].bitcast(I32))
         nc.sync.dma_start(bw_win[:], book_words[0].rearrange("p c t -> p (c t)").bitcast(I32))
         for v in range(4):
@@ -69,24 +69,18 @@ def tile_attend_pqresid_kernel(tc, query, book_words, book_scales, fine_words, f
         vals_rows = vals.rearrange("(p j) e -> p j e", j=4)
         v_first = shared.tile([P, 4, FIRST], F32, name="v_first", align_bytes=64, offset=0)
         nc.sync.dma_start(v_first[:], vals_rows[:, :, 0:FIRST])
+        size_col = shared.tile([P, 4], F32, name="size_col", align_bytes=64, offset=16 * FIRST)
+        nc.sync.dma_start(size_col[:], size.rearrange("o (s t) -> (o s) t", t=4))
 
         q_bf = sb.tile([P, Q, 4], BF16, name="q_bf", align_bytes=64)
         nc.scalar.activation(q_bf[:].rearrange("p (c i) j -> p c j i", i=4), q_raw[:].rearrange("p j (c i) -> p c j i", i=4), ACT.Copy)
-        size_col = sb.tile([P, 4], F32, name="size_col", tag="query_then_size", align_bytes=64)
-        nc.scalar.dma_start(size_col[:], size.rearrange("o (s t) -> (o s) t", t=4))
-        size_ps = ps.tile([P, 2, 2, P], F32, name="size_ps")
-        for u in range(2):
-            for e in range(2):
-                t = 2 * u + e
-                nc.tensor.transpose(size_ps[:, e, u, :], size_col[:, t:t + 1].to_broadcast([P, P]), ident[:])
-
-        v_rest = shared.tile([P, 4, E - FIRST], F32, name="v_rest", align_bytes=64, offset=16 * FIRST)
+        v_rest = shared.tile([P, 4, E - FIRST], F32, name="v_rest", align_bytes=64, offset=16 * FIRST + 64)
         nc.sync.dma_start(v_rest[:], vals_rows[:, :, FIRST:E])
         q_codes = sb.tile([P, Q], U32, name="q_codes", align_bytes=64)
         q_scales = sb.tile([P, Q], U8, name="q_scales", align_bytes=64)
         nc.vector.quantize_mx(out=q_codes[:].bitcast(FP8X4), scales=q_scales[:], in_=q_bf[:].rearrange("p q j -> p (q j)"))
 
-        scores = [ps.tile([P, SLOTS], F32, name="scores%d" % h) for h in range(2)]
+        scores = [ps.tile([P, SLOTS], F32, name="scores%d" % h, tag="scores%d" % h) for h in range(2)]
         for h in range(2):
             cols = slice(h * SLOTS, (h + 1) * SLOTS)
             nc.tensor.matmul_mx(out=scores[h][:], lhsT=q_codes[:].bitcast(FP8X4), lhsT_scale=q_scales[:],
@@ -104,6 +98,12 @@ def tile_attend_pqresid_kernel(tc, query, book_words, book_scales, fine_words, f
                                     scores[h][:].rearrange("p (s u e) -> p u s e", u=2, e=2),
                                     -1.0, start, ALU.mult, ALU.min, accum_out=found)
 
+        size_ps = ps.tile([P, 2, 2, P], F32, name="size_ps", tag="scores0")
+        for u in range(2):
+            for e in range(2):
+                t = 2 * u + e
+                nc.tensor.transpose(size_ps[:, e, u, :], size_col[:, t:t + 1].to_broadcast([P, P]), ident[:])
+
         v_bf0 = sb.tile([P, ON_SCALAR, 4], BF16, name="v_bf0", align_bytes=64)
         nc.scalar.copy(v_bf0[:].rearrange("p (c i) j -> p c j i", i=4), v_first[:, :, 0:ON_SCALAR].rearrange("p j (c i) -> p c j i", i=4))
         v_codes = [shared.tile([P, HALF], U32, name="v_codes0", align_bytes=64, offset=KEYS_AT),
@@ -111,7 +111,7 @@ def tile_attend_pqresid_kernel(tc, query, book_words, book_scales, fine_words, f
         v_scales = [sb.tile([P, HALF], U8, name="v_scales%d" % h, align_bytes=64) for h in range(2)]
         v_bf2 = shared.tile([P, HALF - ON_SCALAR, 4], BF16, name="v_bf2", align_bytes=64, offset=KEYS_AT + 4 * HALF)
         nc.vector.tensor_copy(v_bf2[:].rearrange("p (c i) j -> p c j i", i=4), v_first[:, :, ON_SCALAR:HALF].rearrange("p j (c i) -> p c j i", i=4))
-        for lo, hi, src in ((0, 128, v_bf0[:, 0:128, :]), (128, ON_SCALAR, v_bf0[:, 128:ON_SCALAR, :]), (ON_SCALAR, HALF, v_bf2[:])):
+        for lo, hi, src in ((0, ON_SCALAR, v_bf0[:]), (ON_SCALAR, HALF, v_bf2[:])):
             nc.vector.quantize_mx(out=v_codes[0][:, lo:hi].bitcast(FP8X4), scales=v_scales[0][:, lo:hi], in_=src.rearrange("p e j -> p (e j)"))
         prob = sb.tile([P, 2, P, 2], F32, name="prob", align_bytes=64)
         row_sum = sb.tile([P, 1], F32, name="row_sum")

@@ -23,6 +23,7 @@ KEYS_AT = 16 * E + 64
 SLOTS = I // 2
 LIST_COLS = SLOTS // 16
 PIECE = 128
+EARLY = 768
 
 
 def tile_attend_pqresid_kernel(tc, query, book_words, book_scales, fine_words, fine_scales, size, vals, offs, offs2, out):
@@ -47,9 +48,12 @@ def tile_attend_pqresid_kernel(tc, query, book_words, book_scales, fine_words, f
         nc.sync.dma_start(fine_list[:], offs2)
         nc.sync.dma_start(bs_win[0:P:8, :].bitcast(I32), book_scales[0].bitcast(I32))
         nc.sync.dma_start(bw_win[:], book_words[0].rearrange("p c t -> p (c t)").bitcast(I32))
+        fine_rows = fine_words[0].rearrange("p c t -> p (c t)").bitcast(I32)
         for v in range(4):
+            if v == 2:
+                nc.sync.dma_start(fw_win[:, 0:EARLY], fine_rows[:, 0:EARLY])
             nc.sync.dma_start(fs_win[v:P:32, :].bitcast(I32), fine_scales[0, v:16:4, :].bitcast(I32))
-        nc.sync.dma_start(fw_win[:], fine_words[0].rearrange("p c t -> p (c t)").bitcast(I32))
+        nc.sync.dma_start(fw_win[:, EARLY:T], fine_rows[:, EARLY:T])
 
         ident = sb.tile([P, P], F32, name="ident")
         bs_pl = sb.tile([P, I], U8, name="bs_pl", align_bytes=64)

@@ -23,7 +23,6 @@ KEYS_AT = 16 * E + 64
 SLOTS = I // 2
 LIST_COLS = SLOTS // 16
 PIECE = 128
-EARLY = 768
 
 
 def tile_attend_pqresid_kernel(tc, query, book_words, book_scales, fine_words, fine_scales, size, vals, offs, offs2, out):
@@ -35,8 +34,8 @@ def tile_attend_pqresid_kernel(tc, query, book_words, book_scales, fine_words, f
 
         book_list = sb.tile([P, I // 16], U16, name="book_list")
         fine_list = sb.tile([P, I // 16], U16, name="fine_list")
-        bs_win = shared.tile([P, C], U8, name="bs_win", align_bytes=64, offset=16 * FIRST - C // 2)
-        fs_win = sb.tile([P, T], U8, name="fs_win", align_bytes=64)
+        bs_win = sb.tile([P, C], U8, name="bs_win", align_bytes=64)
+        fs_win = shared.tile([P, T], U8, name="fs_win", align_bytes=64, offset=16 * FIRST - T // 2)
         bw_win = sb.tile([P, C], I32, name="bw_win", align_bytes=64)
         fw_win = sb.tile([P, T], I32, name="fw_win", align_bytes=64)
         q_raw = sb.tile([P, 4, Q], F32, name="q_raw", align_bytes=64)
@@ -47,29 +46,24 @@ def tile_attend_pqresid_kernel(tc, query, book_words, book_scales, fine_words, f
         nc.sync.dma_start(book_list[:], offs)
         nc.sync.dma_start(fine_list[:], offs2)
         nc.sync.dma_start(bs_win[0:P:8, :].bitcast(I32), book_scales[0].bitcast(I32))
+        nc.sync.dma_start(fs_win[0:P:8, :].bitcast(I32), fine_scales[0].bitcast(I32))
         nc.sync.dma_start(bw_win[:], book_words[0].rearrange("p c t -> p (c t)").bitcast(I32))
-        fine_rows = fine_words[0].rearrange("p c t -> p (c t)").bitcast(I32)
-        for v in range(4):
-            if v == 2:
-                nc.sync.dma_start(fw_win[:, 0:EARLY], fine_rows[:, 0:EARLY])
-            nc.sync.dma_start(fs_win[v:P:32, :].bitcast(I32), fine_scales[0, v:16:4, :].bitcast(I32))
-        nc.sync.dma_start(fw_win[:, EARLY:T], fine_rows[:, EARLY:T])
+        nc.sync.dma_start(fw_win[:], fine_words[0].rearrange("p c t -> p (c t)").bitcast(I32))
 
         ident = sb.tile([P, P], F32, name="ident")
-        bs_pl = sb.tile([P, I], U8, name="bs_pl", align_bytes=64)
-        nc.vector.memset(bs_pl[:].bitcast(I32), 0)
+        planes = sb.tile([P, 2 * I], U8, name="planes", align_bytes=64)
+        nc.vector.memset(planes[:].bitcast(I32), 0)
         nc.vector.memset(ident[:], 0.0)
         make_identity(nc, ident[:], nomemset=True)
 
-        bs_g = sb.tile([P, I], U8, name="bs_g", align_bytes=64)
-        fs_g = sb.tile([P, I], U8, name="fs_g", align_bytes=64)
+        bytes_g = sb.tile([P, 2 * I], U8, name="bytes_g", align_bytes=64)
         bw_g = sb.tile([P, I], I32, name="bw_g", align_bytes=64)
         fw_g = shared.tile([P, I], I32, name="fw_g", align_bytes=64, offset=KEYS_AT)
-        nc.vector.tensor_copy(bs_g[:], bs_win[:].indirect(book_list[:]))
+        nc.vector.tensor_copy(bytes_g[:, 0:I], bs_win[:].indirect(book_list[:]))
+        nc.vector.tensor_copy(bytes_g[:, I:2 * I], fs_win[:].indirect(fine_list[:]))
         for x in range(4):
-            nc.sync.dma_start(bs_pl[32 * x:32 * x + 4, :].bitcast(I32), bs_g[32 * x:32 * x + 32:8, :].bitcast(I32))
+            (nc.sync, nc.scalar)[x % 2].dma_start(planes[32 * x:32 * x + 4, :].bitcast(I32), bytes_g[32 * x:32 * x + 32:8, :].bitcast(I32))
         nc.vector.tensor_copy(bw_g[:].bitcast(U32), bw_win[:].bitcast(U32).indirect(book_list[:]))
-        nc.vector.tensor_copy(fs_g[:], fs_win[:].indirect(fine_list[:]))
         vals_rows = vals.rearrange("(p j) e -> p j e", j=4)
         v_first = shared.tile([P, 4, FIRST], F32, name="v_first", align_bytes=64, offset=0)
         nc.sync.dma_start(v_first[:], vals_rows[:, :, 0:FIRST])
@@ -88,11 +82,11 @@ def tile_attend_pqresid_kernel(tc, query, book_words, book_scales, fine_words, f
         for h in range(2):
             cols = slice(h * SLOTS, (h + 1) * SLOTS)
             nc.tensor.matmul_mx(out=scores[h][:], lhsT=q_codes[:].bitcast(FP8X4), lhsT_scale=q_scales[:],
-                                rhs=bw_g[:, cols].bitcast(FP8X4), rhs_scale=bs_pl[:, cols], start=True, stop=False)
+                                rhs=bw_g[:, cols].bitcast(FP8X4), rhs_scale=planes[:, cols], start=True, stop=False)
             nc.vector.tensor_copy(fw_g[:, cols].bitcast(U32),
                                   fw_win[:].bitcast(U32).indirect(fine_list[:, h * LIST_COLS:(h + 1) * LIST_COLS]))
             nc.tensor.matmul_mx(out=scores[h][:], lhsT=q_codes[:].bitcast(FP8X4), lhsT_scale=q_scales[:],
-                                rhs=fw_g[:, cols].bitcast(FP8X4), rhs_scale=fs_g[:, cols], start=False, stop=True)
+                                rhs=fw_g[:, cols].bitcast(FP8X4), rhs_scale=planes[:, I + h * SLOTS:I + (h + 1) * SLOTS], start=False, stop=True)
 
         neg_max0 = sb.tile([P, 1], F32, name="neg_max0")
         neg_max = sb.tile([P, 1], F32, name="neg_max")

@@ -18,11 +18,11 @@ ACT = mybir.ActivationFunctionType
 P = 128
 HALF = E // 2
 FIRST = 256
-ON_SCALAR = 128
 KEYS_AT = 16 * E + 64
 SLOTS = I // 2
 LIST_COLS = SLOTS // 16
 PIECE = 128
+EARLY = 384
 
 
 def tile_attend_pqresid_kernel(tc, query, book_words, book_scales, fine_words, fine_scales, size, vals, offs, offs2, out):
@@ -42,13 +42,15 @@ def tile_attend_pqresid_kernel(tc, query, book_words, book_scales, fine_words, f
 
         nc.vector.memset(bs_win[:].bitcast(I32), 0)
         nc.vector.memset(fs_win[:].bitcast(I32), 0)
-        nc.sync.dma_start(q_raw[:], query.rearrange("(p j) q -> p j q", j=4))
+        fine_rows = fine_words[0].rearrange("p c t -> p (c t)").bitcast(I32)
+        nc.sync.dma_start(fw_win[:, 0:EARLY], fine_rows[:, 0:EARLY])
         nc.sync.dma_start(book_list[:], offs)
-        nc.sync.dma_start(fine_list[:], offs2)
         nc.sync.dma_start(bs_win[0:P:8, :].bitcast(I32), book_scales[0].bitcast(I32))
+        nc.sync.dma_start(q_raw[:], query.rearrange("(p j) q -> p j q", j=4))
+        nc.sync.dma_start(fine_list[:], offs2)
         nc.sync.dma_start(fs_win[0:P:8, :].bitcast(I32), fine_scales[0].bitcast(I32))
         nc.sync.dma_start(bw_win[:], book_words[0].rearrange("p c t -> p (c t)").bitcast(I32))
-        nc.sync.dma_start(fw_win[:], fine_words[0].rearrange("p c t -> p (c t)").bitcast(I32))
+        nc.sync.dma_start(fw_win[:, EARLY:T], fine_rows[:, EARLY:T])
 
         ident = sb.tile([P, P], F32, name="ident")
         planes = sb.tile([P, 2 * I], U8, name="planes", align_bytes=64)
@@ -102,16 +104,9 @@ def tile_attend_pqresid_kernel(tc, query, book_words, book_scales, fine_words, f
                 t = 2 * u + e
                 nc.tensor.transpose(size_ps[:, e, u, :], size_col[:, t:t + 1].to_broadcast([P, P]), ident[:])
 
-        v_bf0 = sb.tile([P, ON_SCALAR, 4], BF16, name="v_bf0", align_bytes=64)
-        nc.scalar.copy(v_bf0[:].rearrange("p (c i) j -> p c j i", i=4), v_first[:, :, 0:ON_SCALAR].rearrange("p j (c i) -> p c j i", i=4))
-        v_codes = [shared.tile([P, HALF], U32, name="v_codes0", align_bytes=64, offset=KEYS_AT),
-                   sb.tile([P, HALF], U32, name="v_codes1", align_bytes=64)]
-        v_scales = [sb.tile([P, HALF], U8, name="v_scales%d" % h, align_bytes=64) for h in range(2)]
-        v_bf2 = shared.tile([P, HALF - ON_SCALAR, 4], BF16, name="v_bf2", align_bytes=64, offset=KEYS_AT + 4 * HALF)
-        nc.vector.tensor_copy(v_bf2[:].rearrange("p (c i) j -> p c j i", i=4), v_first[:, :, ON_SCALAR:HALF].rearrange("p j (c i) -> p c j i", i=4))
-        for lo, hi, src in ((0, ON_SCALAR, v_bf0[:]), (ON_SCALAR, HALF, v_bf2[:])):
-            nc.vector.quantize_mx(out=v_codes[0][:, lo:hi].bitcast(FP8X4), scales=v_scales[0][:, lo:hi], in_=src.rearrange("p e j -> p (e j)"))
-        prob = sb.tile([P, 2, P, 2], F32, name="prob", align_bytes=64)
+        v_bf0 = shared.tile([P, HALF, 4], BF16, name="v_bf0", align_bytes=64, offset=KEYS_AT)
+        nc.vector.tensor_copy(v_bf0[:].rearrange("p (c i) j -> p c j i", i=4), v_first[:].rearrange("p j (c i) -> p c j i", i=4))
+        prob = sb.tile([P, 2, P, 2], F32, name="prob", tag="after_weights", align_bytes=64)
         row_sum = sb.tile([P, 1], F32, name="row_sum")
         nc.scalar.activation(prob[:], neg_scores[:], ACT.Exp, bias=neg_max[:], scale=-1.0, accum_out=row_sum[:])
         inv_sum = sb.tile([P, 1], F32, name="inv_sum")
@@ -123,6 +118,10 @@ def tile_attend_pqresid_kernel(tc, query, book_words, book_scales, fine_words, f
                                            size_ps[:, :, u, :].rearrange("p e s -> p s e"), ALU.mult, ALU.mult)
             nc.tensor.transpose(wt_ps[:, u, :], w_bf[:, u, :, :].rearrange("p s e -> p (s e)").bitcast(F32), ident[:])
 
+        v_codes = [sb.tile([P, HALF], U32, name="v_codes0", tag="after_weights", align_bytes=64),
+                   sb.tile([P, HALF], U32, name="v_codes1", align_bytes=64)]
+        v_scales = [sb.tile([P, HALF], U8, name="v_scales%d" % h, align_bytes=64) for h in range(2)]
+        nc.vector.quantize_mx(out=v_codes[0][:].bitcast(FP8X4), scales=v_scales[0][:], in_=v_bf0[:].rearrange("p e j -> p (e j)"))
         v_bf1 = sb.tile([P, HALF, 4], BF16, name="v_bf1", tag="after_exp", align_bytes=64)
         nc.scalar.copy(v_bf1[:].rearrange("p (c i) j -> p c j i", i=4), v_rest[:].rearrange("p j (c i) -> p c j i", i=4))
         nc.vector.quantize_mx(out=v_codes[1][:].bitcast(FP8X4), scales=v_scales[1][:], in_=v_bf1[:].rearrange("p e j -> p (e j)"))

@@ -66,11 +66,11 @@ def tile_attend_pqresid_kernel(tc, query, book_words, book_scales, fine_words, f
         for x in range(4):
             (nc.sync, nc.scalar)[x % 2].dma_start(planes[32 * x:32 * x + 4, :].bitcast(I32), bytes_g[32 * x:32 * x + 32:8, :].bitcast(I32))
         nc.vector.tensor_copy(bw_g[:].bitcast(U32), bw_win[:].bitcast(U32).indirect(book_list[:]))
+        size_col = shared.tile([P, 4], F32, name="size_col", align_bytes=64, offset=16 * FIRST)
+        nc.sync.dma_start(size_col[:], size.rearrange("o (s t) -> (o s) t", t=4))
         vals_rows = vals.rearrange("(p j) e -> p j e", j=4)
         v_first = shared.tile([P, 4, FIRST], F32, name="v_first", align_bytes=64, offset=0)
         nc.sync.dma_start(v_first[:], vals_rows[:, :, 0:FIRST])
-        size_col = shared.tile([P, 4], F32, name="size_col", align_bytes=64, offset=16 * FIRST)
-        nc.sync.dma_start(size_col[:], size.rearrange("o (s t) -> (o s) t", t=4))
 
         q_bf = sb.tile([P, Q, 4], BF16, name="q_bf", align_bytes=64)
         nc.scalar.activation(q_bf[:].rearrange("p (c i) j -> p c j i", i=4), q_raw[:].rearrange("p j (c i) -> p c j i", i=4), ACT.Copy)
@@ -98,11 +98,11 @@ def tile_attend_pqresid_kernel(tc, query, book_words, book_scales, fine_words, f
                                     scores[h][:].rearrange("p (s u e) -> p u s e", u=2, e=2),
                                     -1.0, start, ALU.mult, ALU.min, accum_out=found)
 
-        size_ps = ps.tile([P, 2, 2, P], F32, name="size_ps", tag="scores0")
+        size_ps = [ps.tile([P, 2, P], F32, name="size_ps%d" % u) for u in range(2)]
         for u in range(2):
             for e in range(2):
                 t = 2 * u + e
-                nc.tensor.transpose(size_ps[:, e, u, :], size_col[:, t:t + 1].to_broadcast([P, P]), ident[:])
+                nc.tensor.transpose(size_ps[u][:, e, :], size_col[:, t:t + 1].to_broadcast([P, P]), ident[:])
 
         v_bf0 = shared.tile([P, HALF, 4], BF16, name="v_bf0", align_bytes=64, offset=KEYS_AT)
         nc.vector.tensor_copy(v_bf0[:].rearrange("p (c i) j -> p c j i", i=4), v_first[:].rearrange("p j (c i) -> p c j i", i=4))
@@ -115,7 +115,7 @@ def tile_attend_pqresid_kernel(tc, query, book_words, book_scales, fine_words, f
         wt_ps = ps.tile([P, 2, Q], F32, name="wt_ps")
         for u in range(2):
             nc.vector.scalar_tensor_tensor(w_bf[:, u, :, :], prob[:, u, :, :], inv_sum[:],
-                                           size_ps[:, :, u, :].rearrange("p e s -> p s e"), ALU.mult, ALU.mult)
+                                           size_ps[u][:].rearrange("p e s -> p s e"), ALU.mult, ALU.mult)
             nc.tensor.transpose(wt_ps[:, u, :], w_bf[:, u, :, :].rearrange("p s e -> p (s e)").bitcast(F32), ident[:])
 
         v_codes = [sb.tile([P, HALF], U32, name="v_codes0", tag="after_weights", align_bytes=64),
@@ -137,7 +137,7 @@ def tile_attend_pqresid_kernel(tc, query, book_words, book_scales, fine_words, f
             res = sb.tile([P, HALF], F32, name="res%d" % h, align_bytes=64)
             for c in range(HALF // PIECE):
                 cols = slice(c * PIECE, (c + 1) * PIECE)
-                acc = ps.tile([P, PIECE], F32, name="acc%d" % turn)
+                acc = ps.tile([P, PIECE], F32, name="acc%d" % turn, tag=("acc0", "acc1", "acc2", "scores0")[turn])
                 nc.tensor.matmul_mx(out=acc[:], lhsT=w_codes[:].bitcast(FP8X4), lhsT_scale=w_scales[:],
                                     rhs=v_codes[h][:, cols].bitcast(FP8X4), rhs_scale=v_scales[h][:, cols], start=True, stop=True)
                 (nc.vector.tensor_copy, nc.scalar.copy)[turn % 2](res[:, cols], acc[:])

@@ -15,14 +15,28 @@ U8 = mybir.dt.uint8
 FP8X4 = mybir.dt.float8_e4m3fn_x4
 ALU = mybir.AluOpType
 ACT = mybir.ActivationFunctionType
+
 P = 128
 HALF = E // 2
-FIRST = 256
-KEYS_AT = 16 * E + 64
 SLOTS = I // 2
 LIST_COLS = SLOTS // 16
 PIECE = 128
+Q_HALF = Q // 2
 EARLY = 384
+BESIDE_EXP = 128
+
+SIZE_AT = 16 * HALF
+REST_AT = SIZE_AT + 64
+KEYS_AT = REST_AT + 16 * HALF
+SUM_AT = KEYS_AT + 4096
+
+
+def interleave(copy, dst, src):
+    copy(dst.rearrange("p (c i) t -> p c t i", i=4), src.rearrange("p t (c i) -> p c t i", i=4))
+
+
+def quantize(nc, codes, scales, values):
+    nc.vector.quantize_mx(out=codes.bitcast(FP8X4), scales=scales, in_=values.rearrange("p c t -> p (c t)"))
 
 
 def tile_attend_pqresid_kernel(tc, query, book_words, book_scales, fine_words, fine_scales, size, vals, offs, offs2, out):
@@ -35,7 +49,7 @@ def tile_attend_pqresid_kernel(tc, query, book_words, book_scales, fine_words, f
         book_list = sb.tile([P, I // 16], U16, name="book_list")
         fine_list = sb.tile([P, I // 16], U16, name="fine_list")
         bs_win = sb.tile([P, C], U8, name="bs_win", align_bytes=64)
-        fs_win = shared.tile([P, T], U8, name="fs_win", align_bytes=64, offset=16 * FIRST - T // 2)
+        fs_win = shared.tile([P, T], U8, name="fs_win", align_bytes=64, offset=SIZE_AT - T // 2)
         bw_win = sb.tile([P, C], I32, name="bw_win", align_bytes=64)
         fw_win = sb.tile([P, T], I32, name="fw_win", align_bytes=64)
         q_raw = sb.tile([P, 4, Q], F32, name="q_raw", align_bytes=64)
@@ -46,7 +60,7 @@ def tile_attend_pqresid_kernel(tc, query, book_words, book_scales, fine_words, f
         nc.sync.dma_start(fw_win[:, 0:EARLY], fine_rows[:, 0:EARLY])
         nc.sync.dma_start(book_list[:], offs)
         nc.sync.dma_start(bs_win[0:P:8, :].bitcast(I32), book_scales[0].bitcast(I32))
-        nc.sync.dma_start(q_raw[:], query.rearrange("(p j) q -> p j q", j=4))
+        nc.sync.dma_start(q_raw[:], query.rearrange("(p t) q -> p t q", t=4))
         nc.sync.dma_start(fine_list[:], offs2)
         nc.sync.dma_start(fs_win[0:P:8, :].bitcast(I32), fine_scales[0].bitcast(I32))
         nc.sync.dma_start(bw_win[:], book_words[0].rearrange("p c t -> p (c t)").bitcast(I32))
@@ -64,21 +78,23 @@ def tile_attend_pqresid_kernel(tc, query, book_words, book_scales, fine_words, f
         nc.vector.tensor_copy(bytes_g[:, 0:I], bs_win[:].indirect(book_list[:]))
         nc.vector.tensor_copy(bytes_g[:, I:2 * I], fs_win[:].indirect(fine_list[:]))
         for x in range(4):
-            (nc.sync, nc.scalar)[x % 2].dma_start(planes[32 * x:32 * x + 4, :].bitcast(I32), bytes_g[32 * x:32 * x + 32:8, :].bitcast(I32))
+            queue = (nc.sync, nc.scalar)[x % 2]
+            queue.dma_start(planes[32 * x:32 * x + 4, :].bitcast(I32), bytes_g[32 * x:32 * x + 32:8, :].bitcast(I32))
         nc.vector.tensor_copy(bw_g[:].bitcast(U32), bw_win[:].bitcast(U32).indirect(book_list[:]))
-        size_col = shared.tile([P, 4], F32, name="size_col", align_bytes=64, offset=16 * FIRST)
+
+        size_col = shared.tile([P, 4], F32, name="size_col", align_bytes=64, offset=SIZE_AT)
         nc.sync.dma_start(size_col[:], size.rearrange("o (s t) -> (o s) t", t=4))
-        vals_rows = vals.rearrange("(p j) e -> p j e", j=4)
-        v_first = shared.tile([P, 4, FIRST], F32, name="v_first", align_bytes=64, offset=0)
-        nc.sync.dma_start(v_first[:], vals_rows[:, :, 0:FIRST])
+        vals_rows = vals.rearrange("(s t) e -> s t e", t=4)
+        v_first = shared.tile([P, 4, HALF], F32, name="v_first", align_bytes=64, offset=0)
+        nc.sync.dma_start(v_first[:], vals_rows[:, :, 0:HALF])
 
         q_bf = sb.tile([P, Q, 4], BF16, name="q_bf", align_bytes=64)
-        nc.scalar.activation(q_bf[:].rearrange("p (c i) j -> p c j i", i=4), q_raw[:].rearrange("p j (c i) -> p c j i", i=4), ACT.Copy)
-        v_rest = shared.tile([P, 4, E - FIRST], F32, name="v_rest", align_bytes=64, offset=16 * FIRST + 64)
-        nc.sync.dma_start(v_rest[:], vals_rows[:, :, FIRST:E])
+        interleave(lambda dst, src: nc.scalar.activation(dst, src, ACT.Copy), q_bf[:], q_raw[:])
+        v_rest = shared.tile([P, 4, HALF], F32, name="v_rest", align_bytes=64, offset=REST_AT)
+        nc.sync.dma_start(v_rest[:], vals_rows[:, :, HALF:E])
         q_codes = sb.tile([P, Q], U32, name="q_codes", align_bytes=64)
         q_scales = sb.tile([P, Q], U8, name="q_scales", align_bytes=64)
-        nc.vector.quantize_mx(out=q_codes[:].bitcast(FP8X4), scales=q_scales[:], in_=q_bf[:].rearrange("p q j -> p (q j)"))
+        quantize(nc, q_codes[:], q_scales[:], q_bf[:])
 
         scores = [ps.tile([P, SLOTS], F32, name="scores%d" % h, tag="scores%d" % h) for h in range(2)]
         for h in range(2):
@@ -88,13 +104,14 @@ def tile_attend_pqresid_kernel(tc, query, book_words, book_scales, fine_words, f
             nc.vector.tensor_copy(fw_g[:, cols].bitcast(U32),
                                   fw_win[:].bitcast(U32).indirect(fine_list[:, h * LIST_COLS:(h + 1) * LIST_COLS]))
             nc.tensor.matmul_mx(out=scores[h][:], lhsT=q_codes[:].bitcast(FP8X4), lhsT_scale=q_scales[:],
-                                rhs=fw_g[:, cols].bitcast(FP8X4), rhs_scale=planes[:, I + h * SLOTS:I + (h + 1) * SLOTS], start=False, stop=True)
+                                rhs=fw_g[:, cols].bitcast(FP8X4), rhs_scale=planes[:, I + h * SLOTS:I + (h + 1) * SLOTS],
+                                start=False, stop=True)
 
         neg_max0 = sb.tile([P, 1], F32, name="neg_max0")
         neg_max = sb.tile([P, 1], F32, name="neg_max")
         neg_scores = sb.tile([P, 2, P, 2], F32, name="neg_scores", tag="after_exp", align_bytes=64)
         for h, (start, found) in enumerate(((None, neg_max0[:]), (neg_max0[:], neg_max[:]))):
-            nc.vector.tensor_scalar(neg_scores[:, :, h * 64:(h + 1) * 64, :],
+            nc.vector.tensor_scalar(neg_scores[:, :, h * SLOTS // 4:(h + 1) * SLOTS // 4, :],
                                     scores[h][:].rearrange("p (s u e) -> p u s e", u=2, e=2),
                                     -1.0, start, ALU.mult, ALU.min, accum_out=found)
 
@@ -104,42 +121,52 @@ def tile_attend_pqresid_kernel(tc, query, book_words, book_scales, fine_words, f
                 t = 2 * u + e
                 nc.tensor.transpose(size_ps[u][:, e, :], size_col[:, t:t + 1].to_broadcast([P, P]), ident[:])
 
-        v_bf0 = shared.tile([P, HALF, 4], BF16, name="v_bf0", align_bytes=64, offset=KEYS_AT)
-        nc.vector.tensor_copy(v_bf0[:].rearrange("p (c i) j -> p c j i", i=4), v_first[:].rearrange("p j (c i) -> p c j i", i=4))
-        prob = sb.tile([P, 2, P, 2], F32, name="prob", tag="after_weights", align_bytes=64)
-        row_sum = sb.tile([P, 1], F32, name="row_sum")
-        nc.scalar.activation(prob[:], neg_scores[:], ACT.Exp, bias=neg_max[:], scale=-1.0, accum_out=row_sum[:])
+        v_bf0 = shared.tile([P, BESIDE_EXP, 4], BF16, name="v_bf0", align_bytes=64, offset=KEYS_AT + 4 * SLOTS)
+        interleave(nc.vector.tensor_copy, v_bf0[:], v_first[:, :, 0:BESIDE_EXP])
+
+        prob = sb.tile([P, 2, P, 2], F32, name="prob", align_bytes=64)
+        row_sum = shared.tile([P, 32], F32, name="row_sum", align_bytes=64, offset=SUM_AT)
+        nc.scalar.activation(prob[:], neg_scores[:], ACT.Exp, bias=neg_max[:], scale=-1.0, accum_out=row_sum[:, 0:1])
         inv_sum = sb.tile([P, 1], F32, name="inv_sum")
-        nc.vector.reciprocal(inv_sum[:], row_sum[:])
+        nc.vector.reciprocal(inv_sum[:], row_sum[:, 0:1])
         w_bf = sb.tile([P, 2, P, 2], BF16, name="w_bf", align_bytes=64)
         wt_ps = ps.tile([P, 2, Q], F32, name="wt_ps")
+        sized = sb.tile([P, P, 2], F32, name="sized", align_bytes=64)
+        nc.vector.tensor_tensor(sized[:], prob[:, 1, :, :], size_ps[1][:].rearrange("p e s -> p s e"), ALU.mult)
+        nc.vector.scalar_tensor_tensor(w_bf[:, 0, :, :], prob[:, 0, :, :], inv_sum[:],
+                                       size_ps[0][:].rearrange("p e s -> p s e"), ALU.mult, ALU.mult)
+        nc.vector.tensor_scalar(w_bf[:, 1, :, :], sized[:], inv_sum[:], None, ALU.mult)
         for u in range(2):
-            nc.vector.scalar_tensor_tensor(w_bf[:, u, :, :], prob[:, u, :, :], inv_sum[:],
-                                           size_ps[u][:].rearrange("p e s -> p s e"), ALU.mult, ALU.mult)
             nc.tensor.transpose(wt_ps[:, u, :], w_bf[:, u, :, :].rearrange("p s e -> p (s e)").bitcast(F32), ident[:])
 
-        v_codes = [sb.tile([P, HALF], U32, name="v_codes0", tag="after_weights", align_bytes=64),
+        v_codes = [shared.tile([P, HALF], U32, name="v_codes0", align_bytes=64, offset=SUM_AT + 64),
                    sb.tile([P, HALF], U32, name="v_codes1", align_bytes=64)]
         v_scales = [sb.tile([P, HALF], U8, name="v_scales%d" % h, align_bytes=64) for h in range(2)]
-        nc.vector.quantize_mx(out=v_codes[0][:].bitcast(FP8X4), scales=v_scales[0][:], in_=v_bf0[:].rearrange("p e j -> p (e j)"))
+        v_bf2 = shared.tile([P, HALF - BESIDE_EXP, 4], BF16, name="v_bf2", align_bytes=64,
+                            offset=SUM_AT + 64 - 8 * (HALF - BESIDE_EXP))
+        interleave(nc.vector.tensor_copy, v_bf2[:], v_first[:, :, BESIDE_EXP:HALF])
+        for cols, src in ((slice(0, BESIDE_EXP), v_bf0), (slice(BESIDE_EXP, HALF), v_bf2)):
+            quantize(nc, v_codes[0][:, cols], v_scales[0][:, cols], src[:])
         v_bf1 = sb.tile([P, HALF, 4], BF16, name="v_bf1", tag="after_exp", align_bytes=64)
-        nc.scalar.copy(v_bf1[:].rearrange("p (c i) j -> p c j i", i=4), v_rest[:].rearrange("p j (c i) -> p c j i", i=4))
-        nc.vector.quantize_mx(out=v_codes[1][:].bitcast(FP8X4), scales=v_scales[1][:], in_=v_bf1[:].rearrange("p e j -> p (e j)"))
+        interleave(nc.scalar.copy, v_bf1[:], v_rest[:])
+        quantize(nc, v_codes[1][:], v_scales[1][:], v_bf1[:])
+
         wt_bf = sb.tile([P, Q, 4], BF16, name="wt_bf", align_bytes=64)
-        nc.scalar.copy(wt_bf[:].rearrange("p q j -> p (q j)").bitcast(F32).rearrange("p (q u) -> p q u", u=2),
-                       wt_ps[:].rearrange("p u q -> p q u"))
         w_codes = sb.tile([P, Q], U32, name="w_codes", align_bytes=64)
         w_scales = sb.tile([P, Q], U8, name="w_scales", align_bytes=64)
-        nc.vector.quantize_mx(out=w_codes[:].bitcast(FP8X4), scales=w_scales[:], in_=wt_bf[:].rearrange("p q j -> p (q j)"))
+        for g in range(2):
+            queries = slice(g * Q_HALF, (g + 1) * Q_HALF)
+            nc.scalar.copy(wt_bf[:, queries, :].rearrange("p q t -> p (q t)").bitcast(F32).rearrange("p (q u) -> p q u", u=2),
+                           wt_ps[:, :, queries].rearrange("p u q -> p q u"))
+            quantize(nc, w_codes[:, queries], w_scales[:, queries], wt_bf[:, queries, :])
 
-        turn = 0
+        banks = ("acc0", "acc1", "acc2", "scores0")
         for h, queue in enumerate((nc.sync, nc.scalar)):
             res = sb.tile([P, HALF], F32, name="res%d" % h, align_bytes=64)
-            for c in range(HALF // PIECE):
+            for c, copy in enumerate((nc.vector.tensor_copy, nc.scalar.copy)):
                 cols = slice(c * PIECE, (c + 1) * PIECE)
-                acc = ps.tile([P, PIECE], F32, name="acc%d" % turn, tag=("acc0", "acc1", "acc2", "scores0")[turn])
+                acc = ps.tile([P, PIECE], F32, name="acc%d" % (2 * h + c), tag=banks[2 * h + c])
                 nc.tensor.matmul_mx(out=acc[:], lhsT=w_codes[:].bitcast(FP8X4), lhsT_scale=w_scales[:],
                                     rhs=v_codes[h][:, cols].bitcast(FP8X4), rhs_scale=v_scales[h][:, cols], start=True, stop=True)
-                (nc.vector.tensor_copy, nc.scalar.copy)[turn % 2](res[:, cols], acc[:])
-                turn = turn + 1
+                copy(res[:, cols], acc[:])
             queue.dma_start(out[:, h * HALF:(h + 1) * HALF], res[:])

@@ -19,7 +19,6 @@ ACT = mybir.ActivationFunctionType
 P = 128
 HALF = E // 2
 SLOTS = I // 2
-LIST_COLS = SLOTS // 16
 PIECE = 128
 Q_HALF = Q // 2
 EARLY = 384
@@ -101,11 +100,14 @@ def tile_attend_pqresid_kernel(tc, query, book_words, book_scales, fine_words, f
             cols = slice(h * SLOTS, (h + 1) * SLOTS)
             nc.tensor.matmul_mx(out=scores[h][:], lhsT=q_codes[:].bitcast(FP8X4), lhsT_scale=q_scales[:],
                                 rhs=bw_g[:, cols].bitcast(FP8X4), rhs_scale=planes[:, cols], start=True, stop=False)
-            nc.vector.tensor_copy(fw_g[:, cols].bitcast(U32),
-                                  fw_win[:].bitcast(U32).indirect(fine_list[:, h * LIST_COLS:(h + 1) * LIST_COLS]))
-            nc.tensor.matmul_mx(out=scores[h][:], lhsT=q_codes[:].bitcast(FP8X4), lhsT_scale=q_scales[:],
-                                rhs=fw_g[:, cols].bitcast(FP8X4), rhs_scale=planes[:, I + h * SLOTS:I + (h + 1) * SLOTS],
-                                start=False, stop=True)
+            run = SLOTS // (h + 1)
+            for first in range(cols.start, cols.stop, run):
+                last = first + run
+                nc.vector.tensor_copy(fw_g[:, first:last].bitcast(U32),
+                                      fw_win[:].bitcast(U32).indirect(fine_list[:, first // 16:last // 16]))
+                nc.tensor.matmul_mx(out=scores[h][:, first - cols.start:last - cols.start], lhsT=q_codes[:].bitcast(FP8X4),
+                                    lhsT_scale=q_scales[:], rhs=fw_g[:, first:last].bitcast(FP8X4),
+                                    rhs_scale=planes[:, I + first:I + last], start=False, stop=last == cols.stop)
 
         neg_max0 = sb.tile([P, 1], F32, name="neg_max0")
         neg_max = sb.tile([P, 1], F32, name="neg_max")

@@ -117,11 +117,11 @@ def tile_attend_pqresid_kernel(tc, query, book_words, book_scales, fine_words, f
                                     scores[h][:].rearrange("p (s u e) -> p u s e", u=2, e=2),
                                     -1.0, start, ALU.mult, ALU.min, accum_out=found)
 
-        size_ps = [ps.tile([P, 2, P], F32, name="size_ps%d" % u) for u in range(2)]
+        size_ps = [ps.tile([P, P, 2], F32, name="size_ps%d" % u) for u in range(2)]
         for u in range(2):
             for e in range(2):
                 t = 2 * u + e
-                nc.tensor.transpose(size_ps[u][:, e, :], size_col[:, t:t + 1].to_broadcast([P, P]), ident[:])
+                nc.tensor.transpose(size_ps[u][:, :, e], size_col[:, t:t + 1].to_broadcast([P, P]), ident[:])
 
         v_bf0 = shared.tile([P, BESIDE_EXP, 4], BF16, name="v_bf0", align_bytes=64, offset=KEYS_AT + 4 * SLOTS)
         interleave(nc.vector.tensor_copy, v_bf0[:], v_first[:, :, 0:BESIDE_EXP])
@@ -134,9 +134,9 @@ def tile_attend_pqresid_kernel(tc, query, book_words, book_scales, fine_words, f
         w_bf = sb.tile([P, 2, P, 2], BF16, name="w_bf", align_bytes=64)
         wt_ps = ps.tile([P, 2, Q], F32, name="wt_ps")
         sized = sb.tile([P, P, 2], F32, name="sized", align_bytes=64)
-        nc.vector.tensor_tensor(sized[:], prob[:, 1, :, :], size_ps[1][:].rearrange("p e s -> p s e"), ALU.mult)
+        nc.vector.tensor_tensor(sized[:], prob[:, 1, :, :], size_ps[1][:], ALU.mult)
         nc.vector.scalar_tensor_tensor(w_bf[:, 0, :, :], prob[:, 0, :, :], inv_sum[:],
-                                       size_ps[0][:].rearrange("p e s -> p s e"), ALU.mult, ALU.mult)
+                                       size_ps[0][:], ALU.mult, ALU.mult)
         nc.vector.tensor_scalar(w_bf[:, 1, :, :], sized[:], inv_sum[:], None, ALU.mult)
         for u in range(2):
             nc.tensor.transpose(wt_ps[:, u, :], w_bf[:, u, :, :].rearrange("p s e -> p (s e)").bitcast(F32), ident[:])

@@ -163,7 +163,7 @@ def tile_attend_pqresid_kernel(tc, query, book_words, book_scales, fine_words, f
             quantize(nc, w_codes[:, queries], w_scales[:, queries], wt_bf[:, queries, :])
 
         banks = ("acc0", "acc1", "acc2", "scores0")
-        for h, queue in enumerate((nc.sync, nc.scalar)):
+        for h in range(2):
             res = sb.tile([P, HALF], F32, name="res%d" % h, align_bytes=64)
             for c, copy in enumerate((nc.vector.tensor_copy, nc.scalar.copy)):
                 cols = slice(c * PIECE, (c + 1) * PIECE)
@@ -171,4 +171,4 @@ def tile_attend_pqresid_kernel(tc, query, book_words, book_scales, fine_words, f
                 nc.tensor.matmul_mx(out=acc[:], lhsT=w_codes[:].bitcast(FP8X4), lhsT_scale=w_scales[:],
                                     rhs=v_codes[h][:, cols].bitcast(FP8X4), rhs_scale=v_scales[h][:, cols], start=True, stop=True)
                 copy(res[:, cols], acc[:])
-            queue.dma_start(out[:, h * HALF:(h + 1) * HALF], res[:])
+            nc.sync.dma_start(out[:, h * HALF:(h + 1) * HALF], res[:])

@@ -23,9 +23,10 @@ PIECE = 128
 Q_HALF = Q // 2
 EARLY = 384
 BESIDE_EXP = 128
+LINE = 256
 
 SIZE_AT = 16 * HALF
-REST_AT = SIZE_AT + 64
+REST_AT = SIZE_AT + LINE
 KEYS_AT = REST_AT + 16 * HALF
 SUM_AT = KEYS_AT + 4096
 
@@ -47,11 +48,11 @@ def tile_attend_pqresid_kernel(tc, query, book_words, book_scales, fine_words, f
 
         book_list = sb.tile([P, I // 16], U16, name="book_list")
         fine_list = sb.tile([P, I // 16], U16, name="fine_list")
-        bs_win = sb.tile([P, C], U8, name="bs_win", align_bytes=64)
-        fs_win = shared.tile([P, T], U8, name="fs_win", align_bytes=64, offset=SIZE_AT - T // 2)
-        bw_win = sb.tile([P, C], I32, name="bw_win", align_bytes=64)
-        fw_win = sb.tile([P, T], I32, name="fw_win", align_bytes=64)
-        q_raw = sb.tile([P, 4, Q], F32, name="q_raw", align_bytes=64)
+        bs_win = sb.tile([P, C], U8, name="bs_win", align_bytes=LINE)
+        fs_win = shared.tile([P, T], U8, name="fs_win", align_bytes=LINE, offset=SIZE_AT - T // 2)
+        bw_win = sb.tile([P, C], I32, name="bw_win", align_bytes=LINE)
+        fw_win = sb.tile([P, T], I32, name="fw_win", align_bytes=LINE)
+        q_raw = sb.tile([P, 4, Q], F32, name="q_raw", align_bytes=LINE)
 
         nc.vector.memset(bs_win[:].bitcast(I32), 0)
         nc.vector.memset(fs_win[:].bitcast(I32), 0)
@@ -66,12 +67,12 @@ def tile_attend_pqresid_kernel(tc, query, book_words, book_scales, fine_words, f
         nc.sync.dma_start(fw_win[:, EARLY:T], fine_rows[:, EARLY:T])
 
         ident = sb.tile([P, P], F32, name="ident")
-        planes = sb.tile([P, 2 * I], U8, name="planes", align_bytes=64)
+        planes = sb.tile([P, 2 * I], U8, name="planes", align_bytes=LINE)
         nc.vector.memset(planes[:].bitcast(I32), 0)
         nc.vector.memset(ident[:], 0.0)
         make_identity(nc, ident[:], nomemset=True)
 
-        bytes_g = sb.tile([P, 2 * I], U8, name="bytes_g", align_bytes=64)
+        bytes_g = sb.tile([P, 2 * I], U8, name="bytes_g", align_bytes=LINE)
         bw_g = sb.tile([P, I], I32, name="bw_g", align_bytes=64)
         fw_g = shared.tile([P, I], I32, name="fw_g", align_bytes=64, offset=KEYS_AT)
         nc.vector.tensor_copy(bytes_g[:, 0:I], bs_win[:].indirect(book_list[:]))
@@ -81,15 +82,15 @@ def tile_attend_pqresid_kernel(tc, query, book_words, book_scales, fine_words, f
             queue.dma_start(planes[32 * x:32 * x + 4, :].bitcast(I32), bytes_g[32 * x:32 * x + 32:8, :].bitcast(I32))
         nc.vector.tensor_copy(bw_g[:].bitcast(U32), bw_win[:].bitcast(U32).indirect(book_list[:]))
 
-        size_col = shared.tile([P, 4], F32, name="size_col", align_bytes=64, offset=SIZE_AT)
+        size_col = shared.tile([P, 4], F32, name="size_col", align_bytes=LINE, offset=SIZE_AT)
         nc.sync.dma_start(size_col[:], size.rearrange("o (s t) -> (o s) t", t=4))
         vals_rows = vals.rearrange("(s t) e -> s t e", t=4)
-        v_first = shared.tile([P, 4, HALF], F32, name="v_first", align_bytes=64, offset=0)
+        v_first = shared.tile([P, 4, HALF], F32, name="v_first", align_bytes=LINE, offset=0)
         nc.sync.dma_start(v_first[:], vals_rows[:, :, 0:HALF])
 
         q_bf = sb.tile([P, Q, 4], BF16, name="q_bf", align_bytes=64)
         interleave(lambda dst, src: nc.scalar.activation(dst, src, ACT.Copy), q_bf[:], q_raw[:])
-        v_rest = shared.tile([P, 4, HALF], F32, name="v_rest", align_bytes=64, offset=REST_AT)
+        v_rest = shared.tile([P, 4, HALF], F32, name="v_rest", align_bytes=LINE, offset=REST_AT)
         nc.sync.dma_start(v_rest[:], vals_rows[:, :, HALF:E])
         q_codes = sb.tile([P, Q], U32, name="q_codes", align_bytes=64)
         q_scales = sb.tile([P, Q], U8, name="q_scales", align_bytes=64)
@@ -164,7 +165,7 @@ def tile_attend_pqresid_kernel(tc, query, book_words, book_scales, fine_words, f
 
         banks = ("acc0", "acc1", "acc2", "scores0")
         for h in range(2):
-            res = sb.tile([P, HALF], F32, name="res%d" % h, align_bytes=64)
+            res = sb.tile([P, HALF], F32, name="res%d" % h, align_bytes=LINE)
             for c, copy in enumerate((nc.vector.tensor_copy, nc.scalar.copy)):
                 cols = slice(c * PIECE, (c + 1) * PIECE)
                 acc = ps.tile([P, PIECE], F32, name="acc%d" % (2 * h + c), tag=banks[2 * h + c])

@@ -21,7 +21,7 @@ HALF = E // 2
 SLOTS = I // 2
 PIECE = 128
 Q_HALF = Q // 2
-EARLY = 384
+EARLY = 320
 BESIDE_EXP = 128
 LINE = 256
 

@@ -164,12 +164,16 @@ def tile_attend_pqresid_kernel(tc, query, book_words, book_scales, fine_words, f
             quantize(nc, w_codes[:, queries], w_scales[:, queries], wt_bf[:, queries, :])
 
         banks = ("acc0", "acc1", "acc2", "scores0")
+        res = [sb.tile([P, width], F32, name="res%d" % n, align_bytes=LINE) for n, width in enumerate((PIECE, PIECE, HALF))]
         for h in range(2):
-            res = sb.tile([P, HALF], F32, name="res%d" % h, align_bytes=LINE)
             for c, copy in enumerate((nc.vector.tensor_copy, nc.scalar.copy)):
                 cols = slice(c * PIECE, (c + 1) * PIECE)
                 acc = ps.tile([P, PIECE], F32, name="acc%d" % (2 * h + c), tag=banks[2 * h + c])
                 nc.tensor.matmul_mx(out=acc[:], lhsT=w_codes[:].bitcast(FP8X4), lhsT_scale=w_scales[:],
                                     rhs=v_codes[h][:, cols].bitcast(FP8X4), rhs_scale=v_scales[h][:, cols], start=True, stop=True)
-                copy(res[:, cols], acc[:])
-            nc.sync.dma_start(out[:, h * HALF:(h + 1) * HALF], res[:])
+                if h == 0:
+                    copy(res[c][:], acc[:])
+                    nc.sync.dma_start(out[:, cols], res[c][:])
+                else:
+                    copy(res[2][:, cols], acc[:])
+        nc.sync.dma_start(out[:, HALF:E], res[2][:])

@@ -86,12 +86,14 @@ def tile_attend_pqresid_kernel(tc, query, book_words, book_scales, fine_words, f
         nc.sync.dma_start(size_col[:], size.rearrange("o (s t) -> (o s) t", t=4))
         vals_rows = vals.rearrange("(s t) e -> s t e", t=4)
         v_first = shared.tile([P, 4, HALF], F32, name="v_first", align_bytes=LINE, offset=0)
-        nc.sync.dma_start(v_first[:], vals_rows[:, :, 0:HALF])
+        for rows in (slice(0, 2), slice(2, 4)):
+            nc.sync.dma_start(v_first[:, rows, :], vals_rows[:, rows, 0:HALF])
 
         q_bf = sb.tile([P, Q, 4], BF16, name="q_bf", align_bytes=64)
         interleave(lambda dst, src: nc.scalar.activation(dst, src, ACT.Copy), q_bf[:], q_raw[:])
         v_rest = shared.tile([P, 4, HALF], F32, name="v_rest", align_bytes=LINE, offset=REST_AT)
-        nc.sync.dma_start(v_rest[:], vals_rows[:, :, HALF:E])
+        for rows in (slice(0, 2), slice(2, 3), slice(3, 4)):
+            nc.sync.dma_start(v_rest[:, rows, :], vals_rows[:, rows, HALF:E])
         q_codes = sb.tile([P, Q], U32, name="q_codes", align_bytes=64)
         q_scales = sb.tile([P, Q], U8, name="q_scales", align_bytes=64)
         quantize(nc, q_codes[:], q_scales[:], q_bf[:])

@@ -156,7 +156,7 @@ def tile_attend_pqresid_kernel(tc, query, book_words, book_scales, fine_words, f
         interleave(nc.scalar.copy, v_bf1[:], v_rest[:])
         quantize(nc, v_codes[1][:], v_scales[1][:], v_bf1[:])
 
-        wt_bf = sb.tile([P, Q, 4], BF16, name="wt_bf", align_bytes=64)
+        wt_bf = sb.tile([P, Q, 4], BF16, name="wt_bf", tag="after_turned", align_bytes=64)
         w_codes = sb.tile([P, Q], U32, name="w_codes", align_bytes=64)
         w_scales = sb.tile([P, Q], U8, name="w_scales", align_bytes=64)
         for g in range(2):
@@ -164,6 +164,9 @@ def tile_attend_pqresid_kernel(tc, query, book_words, book_scales, fine_words, f
             nc.scalar.copy(wt_bf[:, queries, :].rearrange("p q t -> p (q t)").bitcast(F32).rearrange("p (q u) -> p q u", u=2),
                            wt_ps[:, :, queries].rearrange("p u q -> p q u"))
             quantize(nc, w_codes[:, queries], w_scales[:, queries], wt_bf[:, queries, :])
+
+        warm = sb.tile([P, 8], F32, name="warm", tag="after_turned", align_bytes=64)
+        nc.sync.dma_start(warm[:], ident[:, 0:8])
 
         banks = ("acc0", "acc1", "acc2", "scores0")
         res = [sb.tile([P, width], F32, name="res%d" % n, align_bytes=LINE) for n, width in enumerate((PIECE, PIECE, HALF))]

from contextlib import ExitStack

import concourse.mybir as mybir
from concourse.masks import make_identity

D, C, T, I, Q, E = 512, 1024, 2048, 512, 128, 512
FLOPS = 2 * Q * I * (2 * D + E)

F32 = mybir.dt.float32
BF16 = mybir.dt.bfloat16
I32 = mybir.dt.int32
U32 = mybir.dt.uint32
U16 = mybir.dt.uint16
U8 = mybir.dt.uint8
FP8X4 = mybir.dt.float8_e4m3fn_x4
ALU = mybir.AluOpType
ACT = mybir.ActivationFunctionType

P = 128
HALF = E // 2
SLOTS = I // 2
PIECE = 128
Q_HALF = Q // 2
EARLY = 320
BESIDE_EXP = 128
LINE = 256

SIZE_AT = 16 * HALF
REST_AT = SIZE_AT + LINE
KEYS_AT = REST_AT + 16 * HALF
SUM_AT = KEYS_AT + 4096


def interleave(copy, dst, src):
    copy(dst.rearrange("p (c i) t -> p c t i", i=4), src.rearrange("p t (c i) -> p c t i", i=4))


def quantize(nc, codes, scales, values):
    nc.vector.quantize_mx(out=codes.bitcast(FP8X4), scales=scales, in_=values.rearrange("p c t -> p (c t)"))


def tile_attend_pqresid_kernel(tc, query, book_words, book_scales, fine_words, fine_scales, size, vals, offs, offs2, out):
    nc = tc.nc
    with ExitStack() as ctx:
        sb = ctx.enter_context(tc.tile_pool(name="sb", bufs=1))
        shared = ctx.enter_context(tc.tile_pool(name="shared", bufs=1))
        ps = ctx.enter_context(tc.psum_pool(name="ps", bufs=1))

        book_list = sb.tile([P, I // 16], U16, name="book_list")
        fine_list = sb.tile([P, I // 16], U16, name="fine_list")
        bs_win = sb.tile([P, C], U8, name="bs_win", align_bytes=LINE)
        fs_win = shared.tile([P, T], U8, name="fs_win", align_bytes=LINE, offset=SIZE_AT - T // 2)
        bw_win = sb.tile([P, C], I32, name="bw_win", align_bytes=LINE)
        fw_win = sb.tile([P, T], I32, name="fw_win", align_bytes=LINE)
        q_raw = sb.tile([P, 4, Q], F32, name="q_raw", align_bytes=LINE)

        nc.vector.memset(bs_win[:].bitcast(I32), 0)
        nc.vector.memset(fs_win[:].bitcast(I32), 0)
        fine_rows = fine_words[0].rearrange("p c t -> p (c t)").bitcast(I32)
        nc.sync.dma_start(fw_win[:, 0:EARLY], fine_rows[:, 0:EARLY])
        nc.sync.dma_start(book_list[:], offs)
        nc.sync.dma_start(bs_win[0:P:8, :].bitcast(I32), book_scales[0].bitcast(I32))
        nc.sync.dma_start(q_raw[:], query.rearrange("(p t) q -> p t q", t=4))
        nc.sync.dma_start(fine_list[:], offs2)
        nc.sync.dma_start(fs_win[0:P:8, :].bitcast(I32), fine_scales[0].bitcast(I32))
        nc.sync.dma_start(bw_win[:], book_words[0].rearrange("p c t -> p (c t)").bitcast(I32))
        nc.sync.dma_start(fw_win[:, EARLY:T], fine_rows[:, EARLY:T])

        ident = sb.tile([P, P], F32, name="ident")
        planes = sb.tile([P, 2 * I], U8, name="planes", align_bytes=LINE)
        nc.vector.memset(planes[:].bitcast(I32), 0)
        nc.vector.memset(ident[:], 0.0)
        make_identity(nc, ident[:], nomemset=True)

        bytes_g = sb.tile([P, 2 * I], U8, name="bytes_g", align_bytes=LINE)
        bw_g = sb.tile([P, I], I32, name="bw_g", align_bytes=64)
        fw_g = shared.tile([P, I], I32, name="fw_g", align_bytes=64, offset=KEYS_AT)
        nc.vector.tensor_copy(bytes_g[:, 0:I], bs_win[:].indirect(book_list[:]))
        nc.vector.tensor_copy(bytes_g[:, I:2 * I], fs_win[:].indirect(fine_list[:]))
        for x in range(4):
            queue = (nc.sync, nc.scalar)[x % 2]
            queue.dma_start(planes[32 * x:32 * x + 4, :].bitcast(I32), bytes_g[32 * x:32 * x + 32:8, :].bitcast(I32))
        nc.vector.tensor_copy(bw_g[:].bitcast(U32), bw_win[:].bitcast(U32).indirect(book_list[:]))

        size_col = shared.tile([P, 4], F32, name="size_col", align_bytes=LINE, offset=SIZE_AT)
        nc.sync.dma_start(size_col[:], size.rearrange("o (s t) -> (o s) t", t=4))
        vals_rows = vals.rearrange("(s t) e -> s t e", t=4)
        v_first = shared.tile([P, 4, HALF], F32, name="v_first", align_bytes=LINE, offset=0)
        for rows in (slice(0, 2), slice(2, 4)):
            nc.sync.dma_start(v_first[:, rows, :], vals_rows[:, rows, 0:HALF])

        q_bf = sb.tile([P, Q, 4], BF16, name="q_bf", align_bytes=64)
        interleave(lambda dst, src: nc.scalar.activation(dst, src, ACT.Copy), q_bf[:], q_raw[:])
        v_rest = shared.tile([P, 4, HALF], F32, name="v_rest", align_bytes=LINE, offset=REST_AT)
        for rows in (slice(0, 2), slice(2, 3), slice(3, 4)):
            nc.sync.dma_start(v_rest[:, rows, :], vals_rows[:, rows, HALF:E])
        q_codes = sb.tile([P, Q], U32, name="q_codes", align_bytes=64)
        q_scales = sb.tile([P, Q], U8, name="q_scales", align_bytes=64)
        quantize(nc, q_codes[:], q_scales[:], q_bf[:])

        scores = [ps.tile([P, SLOTS], F32, name="scores%d" % h, tag="scores%d" % h) for h in range(2)]
        for h in range(2):
            cols = slice(h * SLOTS, (h + 1) * SLOTS)
            nc.tensor.matmul_mx(out=scores[h][:], lhsT=q_codes[:].bitcast(FP8X4), lhsT_scale=q_scales[:],
                                rhs=bw_g[:, cols].bitcast(FP8X4), rhs_scale=planes[:, cols], start=True, stop=False)
            run = SLOTS // (h + 1)
            for first in range(cols.start, cols.stop, run):
                last = first + run
                nc.vector.tensor_copy(fw_g[:, first:last].bitcast(U32),
                                      fw_win[:].bitcast(U32).indirect(fine_list[:, first // 16:last // 16]))
                nc.tensor.matmul_mx(out=scores[h][:, first - cols.start:last - cols.start], lhsT=q_codes[:].bitcast(FP8X4),
                                    lhsT_scale=q_scales[:], rhs=fw_g[:, first:last].bitcast(FP8X4),
                                    rhs_scale=planes[:, I + first:I + last], start=False, stop=last == cols.stop)

        neg_max0 = sb.tile([P, 1], F32, name="neg_max0")
        neg_max = sb.tile([P, 1], F32, name="neg_max")
        neg_scores = sb.tile([P, 2, P, 2], F32, name="neg_scores", tag="after_exp", align_bytes=64)
        for h, (start, found) in enumerate(((None, neg_max0[:]), (neg_max0[:], neg_max[:]))):
            nc.vector.tensor_scalar(neg_scores[:, :, h * SLOTS // 4:(h + 1) * SLOTS // 4, :],
                                    scores[h][:].rearrange("p (s u e) -> p u s e", u=2, e=2),
                                    -1.0, start, ALU.mult, ALU.min, accum_out=found)

        size_ps = [ps.tile([P, P, 2], F32, name="size_ps%d" % u) for u in range(2)]
        for u in range(2):
            for e in range(2):
                t = 2 * u + e
                nc.tensor.transpose(size_ps[u][:, :, e], size_col[:, t:t + 1].to_broadcast([P, P]), ident[:])

        v_bf0 = shared.tile([P, BESIDE_EXP, 4], BF16, name="v_bf0", align_bytes=64, offset=KEYS_AT + 4 * SLOTS)
        interleave(nc.vector.tensor_copy, v_bf0[:], v_first[:, :, 0:BESIDE_EXP])

        prob = sb.tile([P, 2, P, 2], F32, name="prob", align_bytes=64)
        row_sum = shared.tile([P, 32], F32, name="row_sum", align_bytes=64, offset=SUM_AT)
        nc.scalar.activation(prob[:], neg_scores[:], ACT.Exp, bias=neg_max[:], scale=-1.0, accum_out=row_sum[:, 0:1])
        inv_sum = sb.tile([P, 1], F32, name="inv_sum")
        nc.vector.reciprocal(inv_sum[:], row_sum[:, 0:1])
        w_bf = sb.tile([P, 2, P, 2], BF16, name="w_bf", align_bytes=64)
        wt_ps = ps.tile([P, 2, Q], F32, name="wt_ps")
        sized = sb.tile([P, P, 2], F32, name="sized", align_bytes=64)
        nc.vector.tensor_tensor(sized[:], prob[:, 1, :, :], size_ps[1][:], ALU.mult)
        nc.vector.scalar_tensor_tensor(w_bf[:, 0, :, :], prob[:, 0, :, :], inv_sum[:],
                                       size_ps[0][:], ALU.mult, ALU.mult)
        nc.vector.tensor_scalar(w_bf[:, 1, :, :], sized[:], inv_sum[:], None, ALU.mult)
        for u in range(2):
            nc.tensor.transpose(wt_ps[:, u, :], w_bf[:, u, :, :].rearrange("p s e -> p (s e)").bitcast(F32), ident[:])

        v_codes = [shared.tile([P, HALF], U32, name="v_codes0", align_bytes=64, offset=SUM_AT + 64),
                   sb.tile([P, HALF], U32, name="v_codes1", align_bytes=64)]
        v_scales = [sb.tile([P, HALF], U8, name="v_scales%d" % h, align_bytes=64) for h in range(2)]
        v_bf2 = shared.tile([P, HALF - BESIDE_EXP, 4], BF16, name="v_bf2", align_bytes=64,
                            offset=SUM_AT + 64 - 8 * (HALF - BESIDE_EXP))
        interleave(nc.vector.tensor_copy, v_bf2[:], v_first[:, :, BESIDE_EXP:HALF])
        for cols, src in ((slice(0, BESIDE_EXP), v_bf0), (slice(BESIDE_EXP, HALF), v_bf2)):
            quantize(nc, v_codes[0][:, cols], v_scales[0][:, cols], src[:])
        v_bf1 = sb.tile([P, HALF, 4], BF16, name="v_bf1", tag="after_exp", align_bytes=64)
        interleave(nc.scalar.copy, v_bf1[:], v_rest[:])
        quantize(nc, v_codes[1][:], v_scales[1][:], v_bf1[:])

        wt_bf = sb.tile([P, Q, 4], BF16, name="wt_bf", tag="after_turned", align_bytes=64)
        w_codes = sb.tile([P, Q], U32, name="w_codes", align_bytes=64)
        w_scales = sb.tile([P, Q], U8, name="w_scales", align_bytes=64)
        for g in range(2):
            queries = slice(g * Q_HALF, (g + 1) * Q_HALF)
            nc.scalar.copy(wt_bf[:, queries, :].rearrange("p q t -> p (q t)").bitcast(F32).rearrange("p (q u) -> p q u", u=2),
                           wt_ps[:, :, queries].rearrange("p u q -> p q u"))
            quantize(nc, w_codes[:, queries], w_scales[:, queries], wt_bf[:, queries, :])

        warm = sb.tile([P, 8], F32, name="warm", tag="after_turned", align_bytes=64)
        nc.sync.dma_start(warm[:], ident[:, 0:8])

        banks = ("acc0", "acc1", "acc2", "scores0")
        res = [sb.tile([P, width], F32, name="res%d" % n, align_bytes=LINE) for n, width in enumerate((PIECE, PIECE, HALF))]
        for h in range(2):
            for c, copy in enumerate((nc.vector.tensor_copy, nc.scalar.copy)):
                cols = slice(c * PIECE, (c + 1) * PIECE)
                acc = ps.tile([P, PIECE], F32, name="acc%d" % (2 * h + c), tag=banks[2 * h + c])
                nc.tensor.matmul_mx(out=acc[:], lhsT=w_codes[:].bitcast(FP8X4), lhsT_scale=w_scales[:],
                                    rhs=v_codes[h][:, cols].bitcast(FP8X4), rhs_scale=v_scales[h][:, cols], start=True, stop=True)
                if h == 0:
                    copy(res[c][:], acc[:])
                    nc.sync.dma_start(out[:, cols], res[c][:])
                else:
                    copy(res[2][:, cols], acc[:])
        nc.sync.dma_start(out[:, HALF:E], res[2][:])
